import numpy as np, ml_dtypes
CORES = [3,7,11,15,131,135,139,143]
N = 8
BF = ml_dtypes.bfloat16
L, S, Q = 128, 4, 512
def packed(rng, st):
    fr = np.diff(np.append(st, 2048)); sy = rng.permutation(256)[:len(st)]
    return np.stack([np.repeat(2048 * (fr - 1) + st, fr), np.repeat(sy, fr)])
def model(rng, n):
    return packed(rng, np.concatenate([[0], np.sort(rng.integers(0, 2048 - 8 * n + 1, n - 1)) + 8 * np.arange(1, n)]).astype(np.int64))
def both(m):
    return {"models": np.ascontiguousarray(m[:, :, 0]).astype(np.int32), "letters": np.ascontiguousarray(m[:, :, 1]).astype(np.int32)}
def models_of(rng, n):
    return both(np.stack([np.stack([model(rng, int(n[r, g])) for g in range(8)]) for r in range(N)]))
def some_states(rng):
    return np.clip(np.exp2(12 + 8 * rng.random((N, 8, L))), 4096, 1048575).astype(np.int32)
def some_bytes(rng):
    return rng.integers(0, 256, (N, 8, Q)).astype(np.int32)
def same(p):
    return np.repeat(p[None], N, axis=0).astype(np.int32)
def some_places(rng):
    return same(np.stack([rng.permutation(N * Q) for g in range(8)]))
def setup_inputs(rng):
    n = np.exp2(1 + 6.5 * rng.random((N, 8))).astype(np.int64); n[:, rng.integers(0, 8)] = 256
    m = models_of(rng, n)
    return {"states": some_states(rng), "models": m["models"], "letters": m["letters"], "stock": some_bytes(rng), "places": some_places(rng)}
def setup_inputs_every(rng):
    x = some_states(rng); x[:, :, 0] = 4096; x[:, :, L - 1] = 1048575
    m = models_of(rng, np.full((N, 8), 256)); p = some_places(rng); g = rng.permutation(8)
    p[:, g[0]] = np.arange(N * Q); p[:, g[1]] = np.arange(N * Q)[::-1]
    return {"states": x, "models": m["models"], "letters": m["letters"], "stock": some_bytes(rng), "places": p}
def setup_inputs_dry(rng):
    d = setup_inputs(rng); n = np.exp2(1 + 6.5 * rng.random((N, 8))).astype(np.int64); g = rng.permutation(8); p = rng.permutation(N)
    n[:, g[:3]] = 1
    for i in range(5):
        n[p[i % N], g[3 + i]] = 1
    d.update(models_of(rng, n)); return d
def setup_inputs_edge(rng):
    k = 2 ** rng.integers(4, 11, (N, 8, 1)); up = 4096 // k; a = rng.integers(0, 2048, (N, 8, L)) // k * k
    kind = rng.integers(0, 4, (N, 8, L)); kind[:, :, :4] = np.arange(4)
    x = np.where(kind == 0, 2048 * up + a, np.where(kind == 1, 2048 * (up - 1) + a + k - 1, np.where(kind == 2, 4096, 1048575)))
    m = both(np.stack([np.stack([packed(rng, np.arange(0, 2048, int(k[r, g, 0]))) for g in range(8)]) for r in range(N)]))
    return {"states": x.astype(np.int32), "models": m["models"], "letters": m["letters"], "stock": (255 * rng.integers(0, 2, (N, 8, Q))).astype(np.int32), "places": some_places(rng)}
def setup_inputs_few(rng):
    x = rng.integers(2 ** 19, 2 ** 20, (N, 8, L)); x[:, :, 0] = rng.integers(4096, 8192, (N, 8)); x[:, :, L - 1] = rng.integers(4096, 8192, (N, 8)); x[:, :, 1] = rng.integers(8192, 16384, (N, 8))
    p = rng.permutation(N); m = both(np.stack([np.stack([packed(rng, np.arange(0, 2048, 8 if p[g % N] == r else 1024)) for g in range(8)]) for r in range(N)]))
    return {"states": x.astype(np.int32), "models": m["models"], "letters": m["letters"], "stock": some_bytes(rng), "places": some_places(rng)}
def setup_inputs_spread(rng):
    slot = np.arange(2048); e = np.floor((slot + 1) * rng.random((N, 8, 2048)) ** 3).astype(np.int64); e = np.minimum(e, slot)
    lo = np.maximum(e, 7); w = np.minimum(lo + np.floor((2048 - lo) * rng.random((N, 8, 2048)) ** 4).astype(np.int64), 2047)
    m = 2048 * w + slot - e
    b = np.minimum(np.floor(256 * rng.random((N, 8, Q)) ** 6), 255)
    return {"states": some_states(rng), "models": m.astype(np.int32), "letters": rng.integers(0, 256, (N, 8, 2048)).astype(np.int32), "stock": b.astype(np.int32), "places": some_places(rng)}
def check_inputs(d):
    x, t, a, b, p = d["states"], d["models"].astype(np.int64), d["letters"], d["stock"], d["places"]; bad = []; slot = np.arange(2048)
    if not ((x >= 4096) & (x < 1048576)).all(): bad.append("states")
    if not ((t >= 14336) & (t < 4194304) & ((t & 2047) <= slot) & (slot <= (t & 2047) + (t >> 11))).all(): bad.append("models")
    if not ((a >= 0) & (a < 256)).all(): bad.append("letters")
    if not ((b >= 0) & (b < 256)).all(): bad.append("stock")
    if not ((np.sort(p, axis=2) == np.arange(N * Q)).all() and (p == p[:1]).all()): bad.append("places")
    return bad
def whole(b):
    return np.ascontiguousarray(b.transpose(1, 2, 0)).reshape(8, -1)
def line(v, s):
    return np.ascontiguousarray(v.transpose(1, 0, 2)).reshape(8, -1)
def unline(u, s):
    return u.reshape(8, N, L).transpose(1, 0, 2)
def reference(states, models, letters, stock, places):
    x = states.astype(np.int64); t = models.astype(np.int64); pool = whole(stock.astype(np.int64)); seq = places[0].astype(np.int64)
    syms = np.zeros((N, 8, S * L), np.int32); used = np.zeros(8, np.int64)
    for s in range(S):
        slot = x & 2047; e = np.take_along_axis(t, slot, 2)
        syms[:, :, s * L:(s + 1) * L] = np.take_along_axis(letters, slot, 2)
        x = ((e >> 11) + 1) * (x >> 11) + slot - (e & 2047)
        reads = x < 4096; w = line(reads, s).astype(np.int64)
        at = used[:, None] + np.add.accumulate(w, axis=1) - w
        x = np.where(reads, 256 * x + unline(np.take_along_axis(pool, np.take_along_axis(seq, at, 1), 1), s), x)
        used = used + np.add.reduce(w, axis=1)
    return {"syms": np.asarray(syms, np.float32), "last": np.asarray(x, np.float32)}

@@ -1,0 +1,315 @@
+from concourse.bass import DstId, RemoteDMATransfer
+from concourse.mybir import AluOpType as A, ActivationFunctionType as F
+
+I32, U16, F32, B16 = "int32", "uint16", "float32", "bfloat16"
+SCRATCH = {
+    "snd1": ("dram", [8, 128, 8], I32), "land1": ("dram", [8, 128, 8], I32),
+    "snd2": ("dram", [8, 128, 16], I32), "land2": ("dram", [8, 128, 16], I32),
+    "snd3": ("dram", [8, 128, 16], B16), "land3": ("dram", [8, 128, 16], B16),
+    "snd4": ("dram", [8, 128, 4], F32), "land4": ("dram", [8, 128, 4], F32),
+    "snd5": ("dram", [8, 128, 1], F32), "land5": ("dram", [8, 128, 1], F32),
+    "ia": ("sbuf", [128, 128], I32), "ic": ("sbuf", [128, 128], I32), "ij": ("sbuf", [128, 128], I32),
+    "ip": ("sbuf", [128, 8], I32), "i2": ("sbuf", [128, 8], I32),
+    "cq": ("sbuf", [128, 8], I32), "c7": ("sbuf", [128, 8], I32), "c3": ("sbuf", [128, 8], I32),
+    "qf": ("sbuf", [128, 8], F32), "p15": ("sbuf", [128, 8], F32), "c16": ("sbuf", [128, 8], F32),
+    "pcf": ("sbuf", [128, 8], F32), "permo": ("sbuf", [128, 8], U16),
+    "maskf": ("sbuf", [128, 128], F32), "maskb": ("sbuf", [128, 128], B16),
+    "blkf": ("sbuf", [128, 128], F32), "blkb": ("sbuf", [128, 128], B16),
+    "lt": ("sbuf", [128, 128], B16), "ut": ("sbuf", [128, 128], B16),
+    "sgi": ("sbuf", [128, 128], I32), "sgf": ("sbuf", [128, 128], F32), "e8": ("sbuf", [128, 128], B16),
+    "ones": ("sbuf", [128, 128], B16), "selw": ("sbuf", [128, 1024], B16), "zer": ("sbuf", [128, 8], B16),
+    "i32i": ("sbuf", [128, 32], I32), "i32f": ("sbuf", [128, 32], F32),
+    "ind4i": ("sbuf", [128, 4], I32), "ind4": ("sbuf", [128, 4], F32),
+    "pl": ("sbuf", [128, 32], I32), "zz": ("sbuf", [128, 32], I32), "zh": ("sbuf", [128, 32], I32),
+    "loi": ("sbuf", [128, 32], I32), "lob": ("sbuf", [128, 32], B16), "lor": ("sbuf", [8, 512], B16),
+    "lz": ("sbuf", [128, 256], F32), "offm": ("sbuf", [128, 32], U16), "selm": ("sbuf", [128, 512], B16),
+    "poolw": ("sbuf", [128, 512], I32), "gby": ("sbuf", [128, 512], B16), "bw": ("sbuf", [128, 4112], B16),
+    "wina": ("sbuf", [128, 2048], I32), "win": ("sbuf", [128, 2048], I32),
+    "lti": ("sbuf", [128, 128], I32), "ltb": ("sbuf", [128, 128], B16), "lw": ("sbuf", [128, 2048], B16),
+    "c0": ("sbuf", [128, 8], I32), "x": ("sbuf", [128, 8], I32), "sl": ("sbuf", [128, 8], I32),
+    "off": ("sbuf", [128, 32], U16), "h2": ("sbuf", [128, 8], I32), "g0": ("sbuf", [128, 128], F32),
+    "gm": ("sbuf", [128, 128], F32), "sc": ("sbuf", [128, 128], F32), "f2": ("sbuf", [128, 8], I32),
+    "u": ("sbuf", [128, 8], F32), "pr": ("sbuf", [128, 8], F32), "xp": ("sbuf", [128, 8], F32),
+    "w": ("sbuf", [128, 8], B16), "pp": ("sbuf", [128, 32], B16), "nr": ("sbuf", [128, 8], F32),
+    "pm": ("sbuf", [128, 8], F32), "m": ("sbuf", [128, 8], F32), "n": ("sbuf", [128, 8], F32),
+    "y": ("sbuf", [128, 8], F32), "off2": ("sbuf", [128, 32], U16), "gb": ("sbuf", [128, 128], B16),
+    "sb": ("sbuf", [128, 128], B16), "xl": ("sbuf", [128, 8], F32),
+    "lg": ("sbuf", [128, 512], F32), "outs": ("sbuf", [128, 512], F32),
+    "ps0": ("psum", [128, 512], F32), "ps1": ("psum", [128, 512], F32), "ps2": ("psum", [128, 512], F32),
+    "ps3": ("psum", [128, 512], F32), "ps4": ("psum", [128, 512], F32), "psr": ("psum", [128, 512], F32),
+    "psz": ("psum", [128, 512], F32), "psb": ("psum", [128, 512], F32),
+}
+SEMAPHORES = ["gi", "v", "t", "s", "ls", "a1", "a2", "a3", "a4", "a5",
+              "l1", "l2", "own", "lpl", "lzz", "llt", "dlo", "dlt", "dow3", "dst", "dpa", "dpb", "dwa", "dw", "dlw",
+              "dsy", "dow4", "dla", "dow5", "fsy", "fla"]
+KX = 2047 * 2048
+
+
+def rank_program(g, core, T, topo):
+    me = T.rank_of(core)
+    if me is None:
+        return
+    Q = {"g": g, "v": g.vector, "s": g.scalar, "y": g.sync, "t": g.tensor}
+    cnt, seen, waited = {}, {}, {}
+
+    def did(ins, sem, n=1):
+        ins.then_inc(T.sem[sem], n)
+        cnt[sem] = cnt.get(sem, 0) + n
+        return (sem, cnt[sem])
+
+    def need(q, *toks):
+        for sem, val in toks:
+            if seen.get((q, sem), 0) < val:
+                Q[q].wait_ge(T.sem[sem], val)
+                seen[(q, sem)] = val
+                waited[sem] = max(waited.get(sem, 0), val)
+
+    v, ac, te = g.vector, g.scalar, g.tensor
+
+    def dma(q, out, in_, sem, *toks):
+        need(q, *toks)
+        return did(Q[q].dma_start(out, in_), sem, 16)
+
+    def V(ins):
+        return did(ins, "v")
+
+    def S(ins):
+        return did(ins, "s")
+
+    def P(ins):
+        return did(ins, "t")
+
+    others = [d for d in T.cores if d != core]
+    near = topo.cores_of(core)
+    eng, k, kk = {}, 0, 0
+    for d in others:
+        es = topo.engines(core, d)
+        if d in near:
+            kk += 1
+            eng[d] = es[-kk]
+        else:
+            eng[d] = (es[0::2] + es[1::2])[k]
+            k += 1
+
+    def send(src, dst, arr):
+        tr = []
+        for d in others:
+            rid, pnc = topo.addr(d, core)
+            tr.append(RemoteDMATransfer(dst_ids=[DstId(rid=rid, pnc=pnc)], dma_engine_mask=1 << eng[d],
+                                        remote_sem=T.sem[arr], src=src[T.rank_of(d)], dst=dst[me]))
+        g.remote_dma_fused(tr, local_sem=T.sem.ls)
+        cnt["ls"] = cnt.get("ls", 0) + len(tr)
+        cnt[arr] = len(others)
+        return (arr, len(others))
+
+    dma("y", T.snd1[:, 0:64, :], T.stock[:, :], "l1")
+    dma("y", T.snd1[:, 64:80, :], T.states[:, :], "l1")
+    l1 = dma("y", T.snd1[:, 80:128, :], T.stock[:, 0:384], "l1")
+    l2 = dma("y", T.snd2[:, :, :], T.models[:, :], "l2")
+    dma("y", T.land1[me, 0:64, :], T.stock[me, :], "own")
+    dma("y", T.land1[me, 64:80, :], T.states[me, :], "own")
+    own = dma("y", T.land2[me, :, :], T.models[me, :], "own")
+    lpl = dma("s", T.pl[:, :], T.places[me, :], "lpl")
+    dma("s", T.zz[:, 0:16], T.places[me, 0:2048], "lzz")
+    lzz = dma("s", T.zz[:, 16:32], T.places[me, 2048:4096], "lzz")
+    llt = dma("s", T.lti[:, :], T.letters[:, :], "llt")
+
+    ic = did(g.iota(T.ic[:, :], [[-16, 8], [0, 16]], 0, 1), "gi")
+    ip = did(g.iota(T.ip[:, 0:1], [[0, 1]], 0, 1), "gi")
+    ij = did(g.iota(T.ij[:, :], [[0, 8], [1, 16]], 0, 0), "gi")
+    ia = did(g.iota(T.ia[:, :], [[-1, 128]], 0, 1), "gi")
+    i2 = did(g.iota(T.i2[:, :], [[2, 8]], 0, 0), "gi")
+    need("g", l1)
+    a1 = send(T.snd1, T.land1, "a1")
+    need("g", l2)
+    a2 = send(T.snd2, T.land2, "a2")
+
+    ones = V(v.memset(T.ones[:, :], 1.0))
+    mpo = V(v.memset(T.poolw[:, :], 0))
+    mwa = V(v.memset(T.wina[:, :], 0))
+    zer = V(v.memset(T.zer[:, :], 0.0))
+    lz0 = V(v.memset(T.lz[:, :], 0.0))
+    bw0 = V(v.memset(T.bw[:, 0:1], 0.0))
+    need("v", lpl)
+    loi = V(v.tensor_scalar(T.loi[:, :], T.pl[:, :], 7, None, A.bitwise_and))
+    need("v", loi)
+    lob = V(v.tensor_copy(T.lob[:, :], T.loi[:, :]))
+    need("v", ic, ip)
+    p15 = V(v.tensor_scalar(T.p15[:, 0:1], T.ip[:, 0:1], 15.0, None, A.mult))
+    cq = V(v.tensor_scalar(T.cq[:, 0:1], T.ip[:, 0:1], 15, None, A.bitwise_and))
+    sgi = V(v.tensor_scalar(T.sgi[:, :], T.ic[:, :], 4, None, A.arith_shift_right))
+    n4i = V(v.tensor_scalar(T.ind4i[:, :], T.ic[:, 0:128:32], 5, None, A.arith_shift_right))
+    need("v", lzz)
+    zh = V(v.tensor_scalar(T.zh[:, :], T.zz[:, :], 3, None, A.arith_shift_right))
+    need("v", zh)
+    e8 = V(v.tensor_scalar(T.e8[:, :], T.ic[:, :], T.p15[:, 0:1], 0.0, A.add, A.is_equal))
+    qf = V(v.tensor_copy(T.qf[:, 0:1], T.cq[:, 0:1]))
+    sg = V(v.tensor_scalar(T.sgf[:, :], T.sgi[:, :], 0.0, None, A.is_equal))
+    n4 = V(v.tensor_scalar(T.ind4[:, :], T.ind4i[:, :], 0.0, None, A.is_equal))
+    need("v", ia)
+    i3i = V(v.tensor_scalar(T.i32i[:, :], T.ia[:, 0:32], 31, None, A.bitwise_and))
+    need("v", i3i)
+    i3 = V(v.tensor_scalar(T.i32f[:, :], T.i32i[:, :], 0.0, None, A.is_equal))
+    lz = None
+    for b in range(8):
+        h, bb = b // 4, b % 4
+        c = 128 * h + 16 * b
+        lz = V(v.tensor_scalar(T.lz[:, c:c + 16], T.zh[:, 16 * h:16 * h + 16], T.ind4[:, bb:bb + 1], None, A.mult))
+    need("v", llt)
+    ltb = V(v.tensor_copy(T.ltb[:, :], T.lti[:, :]))
+
+    need("t", lz, i3)
+    te.matmul(T.psz[:, 0:32], T.lz[:, 0:128], T.i32f[:, :], True, False)
+    pz = P(te.matmul(T.psz[:, 0:32], T.lz[:, 128:256], T.i32f[:, :], False, True))
+    dlo = dma("y", T.lor[:, :], T.lob[:, :], "dlo", lob)
+    need("t", dlo, e8)
+    plo = P(te.matmul(T.psr[:, :], T.e8[0:8, :], T.lor[:, :], True, True))
+
+    dlt = dma("y", T.snd3[:, :, :], T.ltb[:, :], "dlt", ltb)
+    dow3 = dma("y", T.land3[me, :, :], T.ltb[16 * me:16 * me + 16, :], "dow3")
+    need("g", dlt)
+    a3 = send(T.snd3, T.land3, "a3")
+
+    need("s", ones, sg)
+    se = None
+    for b in range(8):
+        se = S(ac.activation(T.selw[:, 128 * b:128 * b + 128], T.ones[:, :], F.Copy, 0.0, T.sgf[:, 16 * b:16 * b + 1]))
+
+    need("v", ij, qf)
+    mf = V(v.tensor_scalar(T.maskf[:, :], T.ij[:, :], T.qf[:, 0:1], None, A.is_equal))
+    bf = V(v.tensor_scalar(T.blkf[:, :], T.ij[:, :], 0.0, None, A.is_gt))
+    need("s", mf, bf)
+    mb = S(ac.activation(T.maskb[:, :], T.maskf[:, :], F.Copy))
+    bb_ = S(ac.activation(T.blkb[:, :], T.blkf[:, :], F.Copy))
+    need("s", se)
+    S(ac.activation(T.lw[:, 0:1024], T.selw[:, :], F.Copy))
+    lwf = S(ac.activation(T.lw[:, 1024:2048], T.selw[:, :], F.Copy))
+    need("v", pz)
+    offm = V(v.tensor_copy(T.offm[:, :], T.psz[:, 0:32]))
+    ltm = V(v.tensor_scalar(T.lt[:, :], T.ia[:, :], 0.0, None, A.is_lt))
+    utm = V(v.tensor_scalar(T.ut[:, :], T.ia[:, :], 0.0, None, A.is_gt))
+    need("v", plo)
+    selm = V(v.tensor_scalar(T.selm[:, :], T.psr[:, :], T.qf[:, 0:1], None, A.is_equal))
+    V(v.tensor_scalar(T.c7[:, 0:1], T.ip[:, 0:1], 7, None, A.bitwise_and))
+    c3 = V(v.tensor_scalar(T.c3[:, 0:1], T.ip[:, 0:1], 3, 1, A.arith_shift_right, A.bitwise_and))
+    need("v", c3)
+    c16 = V(v.tensor_scalar(T.c16[:, 0:1], T.c7[:, 0:1], 16.0, None, A.mult))
+    need("v", c16)
+    pcf = V(v.tensor_tensor(T.pcf[:, 0:1], T.c16[:, 0:1], T.c3[:, 0:1], A.add))
+    need("v", pcf, i2)
+    permo = V(v.tensor_scalar(T.permo[:, :], T.i2[:, :], T.pcf[:, 0:1], None, A.add))
+
+    need("y", a1, own, mpo)
+    dst = dma("y", T.c0[:, :], T.land1[:, 64:80, :], "dst")
+    need("s", a1, own, mpo)
+    for b in range(4):
+        dpa = dma("y", T.poolw[16 * b:16 * b + 8, :], T.land1[:, 0:64, :], "dpa")
+        dpb = dma("s", T.poolw[16 * b + 64:16 * b + 72, :], T.land1[:, 0:64, :], "dpb")
+    need("y", a2, mwa)
+    dwa = dma("y", T.wina[0:128:16, :], T.land2[:, :, :], "dwa")
+    for q in range(16):
+        dw = dma("y", T.win[q:128:16, :], T.land2[:, :, :], "dw")
+    dlw = dma("y", T.lw[0:128:16, :], T.land3[:, :, :], "dlw", a3, dow3, lwf)
+
+    need("v", dst)
+    x = V(v.tensor_scalar(T.x[:, :], T.c0[:, :], float(KX), None, A.add))
+    need("v", dpa, dpb, offm, selm)
+    gby = V(v.tensor_tensor(T.gby[:, :], T.poolw[:, :].indirect(T.offm[:, :]), T.selm[:, :], A.mult))
+
+    segc = {}
+
+    def segment(b):
+        ps = T["ps%d" % (b % 5)]
+        need("t", gby, se)
+        if b >= 5:
+            need("t", segc[b - 5])
+        p = P(te.matmul(ps[:, :], T.selw[:, 128 * b:128 * b + 128], T.gby[:, :], True, True))
+        need("s", p)
+        segc[b] = S(ac.activation(T.bw[:, 1 + 512 * b:513 + 512 * b], ps[:, :], F.Copy))
+
+    offs = {}
+
+    def letters(s):
+        need("s", offs[s], dlw, permo)
+        lg = T.lg[:, 128 * s:128 * s + 128]
+        t = S(ac.activation(lg, T.lw[:, :].indirect(T.off[:, 8 * s:8 * s + 8]), F.Copy))
+        need("s", t)
+        lg = T.lg[:, 128 * s:128 * s + 128]
+        return S(ac.activation(T.outs[:, 128 * s:128 * s + 128], lg.indirect(T.permo[:, :]), F.Copy))
+
+    segment(0)
+    segment(1)
+    prev = None
+    outs = None
+    for s in range(4):
+        c = 8 * s
+        need("v", x)
+        t = V(v.tensor_scalar(T.sl[:, :], T.x[:, :], 2047, None, A.bitwise_and))
+        need("v", t)
+        offs[s] = V(v.tensor_copy(T.off[:, c:c + 8], T.sl[:, :]))
+        need("v", offs[s])
+        if s == 0:
+            need("v", dwa)
+            t = V(v.tensor_copy(T.g0[:, :], T.wina[:, :].indirect(T.off[:, c:c + 8])))
+            need("t", t, sg, plo, selm)
+            t = P(te.matmul(T.psr[:, 0:128], T.sgf[:, :], T.g0[:, :], True, True))
+            h2 = V(v.tensor_scalar(T.h2[:, :], T.x[:, :], 2.0 ** -11, 0.500244140625, A.mult, A.add))
+            need("v", t, mf)
+            gm = V(v.tensor_tensor(T.gm[:, :], T.psr[:, 0:128], T.maskf[:, :], A.mult))
+        else:
+            need("v", dw)
+            gm = V(v.tensor_tensor(T.gm[:, :], T.win[:, :].indirect(T.off[:, c:c + 8]), T.maskf[:, :], A.mult))
+            h2 = V(v.tensor_scalar(T.h2[:, :], T.x[:, :], 2.0 ** -11, 0.500244140625, A.mult, A.add))
+        need("v", gm, h2, bf)
+        e = V(v.tensor_tensor_scan(T.sc[:, :], T.blkf[:, :], T.gm[:, :], 0.0, A.mult, A.add))
+        need("v", e)
+        E = T.sc[:, 15:128:16]
+        f2 = V(v.tensor_scalar(T.f2[:, :], E, 2.0 ** -11, -2047.499755859375, A.mult, A.add))
+        u = V(v.tensor_tensor(T.u[:, :], T.x[:, :], E, A.subtract))
+        need("v", u)
+        pr = V(v.tensor_tensor(T.pr[:, :], T.f2[:, :], T.h2[:, :], A.mult))
+        need("v", pr)
+        xp = V(v.tensor_tensor(T.xp[:, :], T.pr[:, :], T.u[:, :], A.add))
+        need("v", xp)
+        w = V(v.tensor_scalar(T.w[:, :], T.xp[:, :], 4096.0, None, A.is_lt))
+        need("v", w, zer)
+        ini = 0.0 if s == 0 else T.pp[:, c - 1:c]
+        pp = V(v.tensor_tensor_scan(T.pp[:, c:c + 8], T.w[:, :], T.zer[:, :], ini, A.add, A.max))
+        if s > 0:
+            need("t", prev, utm)
+            te.matmul(T.psb[:, 0:1], T.ut[:, :], T.pp[:, c - 1:c], True, False)
+        need("t", pp, ltm)
+        base = P(te.matmul(T.psb[:, 0:1], T.lt[:, :], T.pp[:, c + 7:c + 8], s == 0, True))
+        nr = V(v.tensor_scalar(T.nr[:, :], T.xp[:, :], 4096.0, -8192.0, A.is_ge, A.mult))
+        m = V(v.tensor_tensor(T.m[:, :], T.w[:, :], T.xp[:, :], A.mult))
+        need("v", pp, m)
+        pm = V(v.tensor_tensor(T.pm[:, :], T.pp[:, c:c + 8], T.nr[:, :], A.add))
+        n = V(v.tensor_scalar(T.n[:, :], T.m[:, :], 255.0, float(KX if s < 3 else 0), A.mult, A.add))
+        need("v", pm, n)
+        y = V(v.tensor_tensor(T.y[:, :], T.n[:, :], T.xp[:, :], A.add))
+        need("v", base)
+        prev = V(v.tensor_scalar(T.off2[:, c:c + 8], T.pm[:, :], T.psb[:, 0:1], 0.0, A.add, A.max))
+        need("v", prev, mb, bb_, bw0, segc[2 * s + 1])
+        t = V(v.tensor_tensor(T.gb[:, :], T.bw[:, 0:1025 + 1024 * s].indirect(T.off2[:, c:c + 8]), T.maskb[:, :], A.mult))
+        need("v", t)
+        t = V(v.tensor_tensor_scan(T.sb[:, :], T.blkb[:, :], T.gb[:, :], 0.0, A.mult, A.add))
+        need("v", t, y)
+        x = V(v.tensor_tensor(T.x[:, :] if s < 3 else T.xl[:, :], T.y[:, :], T.sb[:, 15:128:16], A.add))
+        if s < 3:
+            segment(2 * s + 2)
+            segment(2 * s + 3)
+        outs = letters(s)
+
+    dsy = dma("s", T.snd4[:, :, :], T.outs[0:128:16, :], "dsy", outs)
+    dow4 = dma("s", T.land4[me, :, :], T.outs[16 * me:16 * me + 1, :], "dow4")
+    need("g", dsy)
+    a4 = send(T.snd4, T.land4, "a4")
+    dla = dma("y", T.snd5[:, :, :], T.xl[:, :], "dla", x)
+    dow5 = dma("y", T.land5[me, :, :], T.xl[16 * me:16 * me + 16, :], "dow5")
+    need("g", dla)
+    a5 = send(T.snd5, T.land5, "a5")
+    dma("s", T.syms[:, :], T.land4[:, :, :], "fsy", a4, dow4)
+    dma("y", T.last[:, :], T.land5[:, :, :], "fla", a5, dow5)
+    for sem in sorted(cnt):
+        if waited.get(sem, 0) < cnt[sem]:
+            need("g", (sem, cnt[sem]))

@@ -2,47 +2,26 @@ from concourse.bass import DstId, RemoteDMATransfer
 from concourse.mybir import AluOpType as A, ActivationFunctionType as F
 
 I32, U16, F32, B16 = "int32", "uint16", "float32", "bfloat16"
-SCRATCH = {
-    "snd1": ("dram", [8, 128, 8], I32), "land1": ("dram", [8, 128, 8], I32),
-    "snd2": ("dram", [8, 128, 16], I32), "land2": ("dram", [8, 128, 16], I32),
-    "snd3": ("dram", [8, 128, 16], B16), "land3": ("dram", [8, 128, 16], B16),
-    "snd4": ("dram", [8, 128, 4], F32), "land4": ("dram", [8, 128, 4], F32),
-    "snd5": ("dram", [8, 128, 1], F32), "land5": ("dram", [8, 128, 1], F32),
-    "ia": ("sbuf", [128, 128], I32), "ic": ("sbuf", [128, 128], I32), "ij": ("sbuf", [128, 128], I32),
-    "ip": ("sbuf", [128, 8], I32), "i2": ("sbuf", [128, 8], I32),
-    "cq": ("sbuf", [128, 8], I32), "c7": ("sbuf", [128, 8], I32), "c3": ("sbuf", [128, 8], I32),
-    "qf": ("sbuf", [128, 8], F32), "p15": ("sbuf", [128, 8], F32), "c16": ("sbuf", [128, 8], F32),
-    "pcf": ("sbuf", [128, 8], F32), "permo": ("sbuf", [128, 8], U16),
-    "maskf": ("sbuf", [128, 128], F32), "maskb": ("sbuf", [128, 128], B16),
-    "blkf": ("sbuf", [128, 128], F32), "blkb": ("sbuf", [128, 128], B16),
-    "lt": ("sbuf", [128, 128], B16), "ut": ("sbuf", [128, 128], B16),
-    "sgi": ("sbuf", [128, 128], I32), "sgf": ("sbuf", [128, 128], F32), "e8": ("sbuf", [128, 128], B16),
-    "ones": ("sbuf", [128, 128], B16), "selw": ("sbuf", [128, 1024], B16), "zer": ("sbuf", [128, 8], B16),
-    "i32i": ("sbuf", [128, 32], I32), "i32f": ("sbuf", [128, 32], F32),
-    "ind4i": ("sbuf", [128, 4], I32), "ind4": ("sbuf", [128, 4], F32),
-    "pl": ("sbuf", [128, 32], I32), "zz": ("sbuf", [128, 32], I32), "zh": ("sbuf", [128, 32], I32),
-    "loi": ("sbuf", [128, 32], I32), "lob": ("sbuf", [128, 32], B16), "lor": ("sbuf", [8, 512], B16),
-    "lz": ("sbuf", [128, 256], F32), "offm": ("sbuf", [128, 32], U16), "selm": ("sbuf", [128, 512], B16),
-    "poolw": ("sbuf", [128, 512], I32), "gby": ("sbuf", [128, 512], B16), "bw": ("sbuf", [128, 4112], B16),
-    "wina": ("sbuf", [128, 2048], I32), "win": ("sbuf", [128, 2048], I32),
-    "lti": ("sbuf", [128, 128], I32), "ltb": ("sbuf", [128, 128], B16), "lw": ("sbuf", [128, 2048], B16),
-    "c0": ("sbuf", [128, 8], I32), "x": ("sbuf", [128, 8], I32), "sl": ("sbuf", [128, 8], I32),
-    "off": ("sbuf", [128, 32], U16), "h2": ("sbuf", [128, 8], I32), "g0": ("sbuf", [128, 128], F32),
-    "gm": ("sbuf", [128, 128], F32), "sc": ("sbuf", [128, 128], F32), "f2": ("sbuf", [128, 8], I32),
-    "u": ("sbuf", [128, 8], F32), "pr": ("sbuf", [128, 8], F32), "xp": ("sbuf", [128, 8], F32),
-    "w": ("sbuf", [128, 8], B16), "pp": ("sbuf", [128, 32], B16), "nr": ("sbuf", [128, 8], F32),
-    "pm": ("sbuf", [128, 8], F32), "m": ("sbuf", [128, 8], F32), "n": ("sbuf", [128, 8], F32),
-    "y": ("sbuf", [128, 8], F32), "off2": ("sbuf", [128, 32], U16), "gb": ("sbuf", [128, 128], B16),
-    "sb": ("sbuf", [128, 128], B16), "xl": ("sbuf", [128, 8], F32),
-    "lg": ("sbuf", [128, 512], F32), "outs": ("sbuf", [128, 512], F32),
-    "ps0": ("psum", [128, 512], F32), "ps1": ("psum", [128, 512], F32), "ps2": ("psum", [128, 512], F32),
-    "ps3": ("psum", [128, 512], F32), "ps4": ("psum", [128, 512], F32), "psr": ("psum", [128, 512], F32),
-    "psz": ("psum", [128, 512], F32), "psb": ("psum", [128, 512], F32),
-}
+SCRATCH = {}
+for _i, _w, _t in ((1, 8, I32), (2, 16, I32), (3, 16, B16), (4, 4, F32), (5, 1, F32)):
+    SCRATCH["snd%d" % _i] = SCRATCH["land%d" % _i] = ("dram", [8, 128, _w], _t)
+for _t, _l in (
+        (I32, "ia 128 ic 128 ij 128 ip 8 i2 8 cq 8 c7 8 c3 8 sgi 128 i32i 32 ind4i 4 pl 32 zz 32 zh 32 loi 32 poolw 512"
+              " wina 2048 win 2048 lti 128 c0 8 f3 8 h2 8 y 8 ylo 8 sl 8"),
+        (U16, "permo 8 offm 32 off 32 off2 32"),
+        (F32, "qf 8 p15 8 c16 8 pcf 8 maskf 128 blkf 128 sgf 128 i32f 32 ind4 4 lz 256 g0 128 gm 128 sc 128 u 8 pr 8 xq 8"
+              " m 8 n 8 yt 8 xl 8 lg 512 outs 512"),
+        (B16, "maskb 128 blkb 128 lt 128 ut 128 e8 128 ones 128 idn 128 i8k 128 n64 8 selw 1024 zer 8 lob 32 selm 512"
+              " gby 512 bw 4112 ltb 128 lw 2048 w 8 pp 32 sb 128 gb 128")):
+    _l = _l.split()
+    for _i in range(0, len(_l), 2):
+        SCRATCH[_l[_i]] = ("sbuf", [128, int(_l[_i + 1])], _t)
+SCRATCH["lor"] = ("sbuf", [8, 512], B16)
+for _i in ("ps0", "ps1", "ps2", "ps3", "ps4", "psr", "psz", "psb"):
+    SCRATCH[_i] = ("psum", [128, 512], F32)
 SEMAPHORES = ["gi", "v", "t", "s", "ls", "a1", "a2", "a3", "a4", "a5",
               "l1", "l2", "own", "lpl", "lzz", "llt", "dlo", "dlt", "dow3", "dst", "dpa", "dpb", "dwa", "dw", "dlw",
               "dsy", "dow4", "dla", "dow5", "fsy", "fla"]
-KX = 2047 * 2048
 
 
 def rank_program(g, core, T, topo):
@@ -79,6 +58,15 @@ def rank_program(g, core, T, topo):
     def P(ins):
         return did(ins, "t")
 
+    def ts(out, in_, s1, s2, o1, *o2):
+        return V(v.tensor_scalar(out, in_, s1, s2, o1, *o2))
+
+    def tt(out, a, b, op):
+        return V(v.tensor_tensor(out, a, b, op))
+
+    def act(out, in_, *sc):
+        return S(ac.activation(out, in_, F.Copy, *sc))
+
     others = [d for d in T.cores if d != core]
     near = topo.cores_of(core)
     eng, k, kk = {}, 0, 0
@@ -103,21 +91,21 @@ def rank_program(g, core, T, topo):
         return (arr, len(others))
 
     dma("y", T.snd1[:, 0:64, :], T.stock[:, :], "l1")
+    l2 = dma("s", T.snd2[:, :, :], T.models[:, :], "l2")
     dma("y", T.snd1[:, 64:80, :], T.states[:, :], "l1")
     l1 = dma("y", T.snd1[:, 80:128, :], T.stock[:, 0:384], "l1")
-    l2 = dma("y", T.snd2[:, :, :], T.models[:, :], "l2")
-    dma("y", T.land1[me, 0:64, :], T.stock[me, :], "own")
-    dma("y", T.land1[me, 64:80, :], T.states[me, :], "own")
-    own = dma("y", T.land2[me, :, :], T.models[me, :], "own")
     lpl = dma("s", T.pl[:, :], T.places[me, :], "lpl")
     dma("s", T.zz[:, 0:16], T.places[me, 0:2048], "lzz")
     lzz = dma("s", T.zz[:, 16:32], T.places[me, 2048:4096], "lzz")
+    dma("y", T.land1[me, 0:64, :], T.stock[me, :], "own")
+    dma("y", T.land1[me, 64:80, :], T.states[me, :], "own")
+    own = dma("y", T.land2[me, :, :], T.models[me, :], "own")
     llt = dma("s", T.lti[:, :], T.letters[:, :], "llt")
 
     ic = did(g.iota(T.ic[:, :], [[-16, 8], [0, 16]], 0, 1), "gi")
     ip = did(g.iota(T.ip[:, 0:1], [[0, 1]], 0, 1), "gi")
-    ij = did(g.iota(T.ij[:, :], [[0, 8], [1, 16]], 0, 0), "gi")
     ia = did(g.iota(T.ia[:, :], [[-1, 128]], 0, 1), "gi")
+    ij = did(g.iota(T.ij[:, :], [[0, 8], [1, 16]], 0, 0), "gi")
     i2 = did(g.iota(T.i2[:, :], [[2, 8]], 0, 0), "gi")
     need("g", l1)
     a1 = send(T.snd1, T.land1, "a1")
@@ -126,37 +114,44 @@ def rank_program(g, core, T, topo):
 
     ones = V(v.memset(T.ones[:, :], 1.0))
     mpo = V(v.memset(T.poolw[:, :], 0))
-    mwa = V(v.memset(T.wina[:, :], 0))
-    zer = V(v.memset(T.zer[:, :], 0.0))
-    lz0 = V(v.memset(T.lz[:, :], 0.0))
-    bw0 = V(v.memset(T.bw[:, 0:1], 0.0))
-    need("v", lpl)
-    loi = V(v.tensor_scalar(T.loi[:, :], T.pl[:, :], 7, None, A.bitwise_and))
-    need("v", loi)
-    lob = V(v.tensor_copy(T.lob[:, :], T.loi[:, :]))
     need("v", ic, ip)
-    p15 = V(v.tensor_scalar(T.p15[:, 0:1], T.ip[:, 0:1], 15.0, None, A.mult))
-    cq = V(v.tensor_scalar(T.cq[:, 0:1], T.ip[:, 0:1], 15, None, A.bitwise_and))
-    sgi = V(v.tensor_scalar(T.sgi[:, :], T.ic[:, :], 4, None, A.arith_shift_right))
-    n4i = V(v.tensor_scalar(T.ind4i[:, :], T.ic[:, 0:128:32], 5, None, A.arith_shift_right))
-    need("v", lzz)
-    zh = V(v.tensor_scalar(T.zh[:, :], T.zz[:, :], 3, None, A.arith_shift_right))
-    need("v", zh)
-    e8 = V(v.tensor_scalar(T.e8[:, :], T.ic[:, :], T.p15[:, 0:1], 0.0, A.add, A.is_equal))
+    sgi = ts(T.sgi[:, :], T.ic[:, :], 4, None, A.arith_shift_right)
+    p15 = ts(T.p15[:, 0:1], T.ip[:, 0:1], 15.0, None, A.mult)
+    cq = ts(T.cq[:, 0:1], T.ip[:, 0:1], 15, None, A.bitwise_and)
+    n4i = ts(T.ind4i[:, :], T.ic[:, 0:128:32], 5, None, A.arith_shift_right)
+    need("v", n4i)
+    sg = ts(T.sgf[:, :], T.sgi[:, :], 0.0, None, A.is_equal)
+    e8 = ts(T.e8[:, :], T.ic[:, :], T.p15[:, 0:1], 0.0, A.add, A.is_equal)
     qf = V(v.tensor_copy(T.qf[:, 0:1], T.cq[:, 0:1]))
-    sg = V(v.tensor_scalar(T.sgf[:, :], T.sgi[:, :], 0.0, None, A.is_equal))
-    n4 = V(v.tensor_scalar(T.ind4[:, :], T.ind4i[:, :], 0.0, None, A.is_equal))
+    n4 = ts(T.ind4[:, :], T.ind4i[:, :], 0.0, None, A.is_equal)
     need("v", ia)
-    i3i = V(v.tensor_scalar(T.i32i[:, :], T.ia[:, 0:32], 31, None, A.bitwise_and))
-    need("v", i3i)
-    i3 = V(v.tensor_scalar(T.i32f[:, :], T.i32i[:, :], 0.0, None, A.is_equal))
+    i3i = ts(T.i32i[:, :], T.ia[:, 0:32], 31, None, A.bitwise_and)
+    mwa = V(v.memset(T.wina[:, :], 0))
+    i3 = ts(T.i32f[:, :], T.i32i[:, :], 0.0, None, A.is_equal) if not need("v", mwa) else None
+    lz0 = V(v.memset(T.lz[:, :], 0.0))
+    need("v", lpl)
+    loi = ts(T.loi[:, :], T.pl[:, :], 7, None, A.bitwise_and)
+    need("v", lzz)
+    zh = ts(T.zh[:, :], T.zz[:, :], 3, None, A.arith_shift_right)
+    need("v", zh)
+    lob = V(v.tensor_copy(T.lob[:, :], T.loi[:, :]))
     lz = None
     for b in range(8):
         h, bb = b // 4, b % 4
         c = 128 * h + 16 * b
-        lz = V(v.tensor_scalar(T.lz[:, c:c + 16], T.zh[:, 16 * h:16 * h + 16], T.ind4[:, bb:bb + 1], None, A.mult))
+        lz = ts(T.lz[:, c:c + 16], T.zh[:, 16 * h:16 * h + 16], T.ind4[:, bb:bb + 1], None, A.mult)
+    need("v", ij)
+    mf = ts(T.maskf[:, :], T.ij[:, :], T.qf[:, 0:1], None, A.is_equal)
+    bf = ts(T.blkf[:, :], T.ij[:, :], 0.0, None, A.is_gt)
     need("v", llt)
     ltb = V(v.tensor_copy(T.ltb[:, :], T.lti[:, :]))
+    ts(T.lt[:, :], T.ia[:, :], 0.0, None, A.is_lt)
+    ts(T.ut[:, :], T.ia[:, :], 0.0, None, A.is_gt)
+    ts(T.idn[:, :], T.ia[:, :], 0.0, None, A.is_equal)
+    ts(T.i8k[:, :], T.ia[:, :], 0.0, 8192.0, A.is_equal, A.mult)
+    V(v.memset(T.zer[:, :], 0.0))
+    V(v.memset(T.n64[:, :], -64.0))
+    con = V(v.memset(T.bw[:, 0:1], 0.0))
 
     need("t", lz, i3)
     te.matmul(T.psz[:, 0:32], T.lz[:, 0:128], T.i32f[:, :], True, False)
@@ -165,39 +160,30 @@ def rank_program(g, core, T, topo):
     need("t", dlo, e8)
     plo = P(te.matmul(T.psr[:, :], T.e8[0:8, :], T.lor[:, :], True, True))
 
-    dlt = dma("y", T.snd3[:, :, :], T.ltb[:, :], "dlt", ltb)
-    dow3 = dma("y", T.land3[me, :, :], T.ltb[16 * me:16 * me + 16, :], "dow3")
-    need("g", dlt)
-    a3 = send(T.snd3, T.land3, "a3")
+    need("v", pz)
+    offm = V(v.tensor_copy(T.offm[:, :], T.psz[:, 0:32]))
+    ts(T.c7[:, 0:1], T.ip[:, 0:1], 7, None, A.bitwise_and)
+    c3 = ts(T.c3[:, 0:1], T.ip[:, 0:1], 3, 1, A.arith_shift_right, A.bitwise_and)
+    need("v", c3)
+    c16 = ts(T.c16[:, 0:1], T.c7[:, 0:1], 16.0, None, A.mult)
+    need("v", c16)
+    pcf = tt(T.pcf[:, 0:1], T.c16[:, 0:1], T.c3[:, 0:1], A.add)
+    need("v", pcf, i2)
+    permo = ts(T.permo[:, :], T.i2[:, :], T.pcf[:, 0:1], None, A.add)
+    need("v", plo)
+    selm = ts(T.selm[:, :], T.psr[:, :], T.qf[:, 0:1], None, A.is_equal)
 
     need("s", ones, sg)
     se = None
     for b in range(8):
-        se = S(ac.activation(T.selw[:, 128 * b:128 * b + 128], T.ones[:, :], F.Copy, 0.0, T.sgf[:, 16 * b:16 * b + 1]))
-
-    need("v", ij, qf)
-    mf = V(v.tensor_scalar(T.maskf[:, :], T.ij[:, :], T.qf[:, 0:1], None, A.is_equal))
-    bf = V(v.tensor_scalar(T.blkf[:, :], T.ij[:, :], 0.0, None, A.is_gt))
+        se = act(T.selw[:, 128 * b:128 * b + 128], T.ones[:, :], 0.0, T.sgf[:, 16 * b:16 * b + 1])
     need("s", mf, bf)
-    mb = S(ac.activation(T.maskb[:, :], T.maskf[:, :], F.Copy))
-    bb_ = S(ac.activation(T.blkb[:, :], T.blkf[:, :], F.Copy))
-    need("s", se)
-    S(ac.activation(T.lw[:, 0:1024], T.selw[:, :], F.Copy))
-    lwf = S(ac.activation(T.lw[:, 1024:2048], T.selw[:, :], F.Copy))
-    need("v", pz)
-    offm = V(v.tensor_copy(T.offm[:, :], T.psz[:, 0:32]))
-    ltm = V(v.tensor_scalar(T.lt[:, :], T.ia[:, :], 0.0, None, A.is_lt))
-    utm = V(v.tensor_scalar(T.ut[:, :], T.ia[:, :], 0.0, None, A.is_gt))
-    need("v", plo)
-    selm = V(v.tensor_scalar(T.selm[:, :], T.psr[:, :], T.qf[:, 0:1], None, A.is_equal))
-    V(v.tensor_scalar(T.c7[:, 0:1], T.ip[:, 0:1], 7, None, A.bitwise_and))
-    c3 = V(v.tensor_scalar(T.c3[:, 0:1], T.ip[:, 0:1], 3, 1, A.arith_shift_right, A.bitwise_and))
-    need("v", c3)
-    c16 = V(v.tensor_scalar(T.c16[:, 0:1], T.c7[:, 0:1], 16.0, None, A.mult))
-    need("v", c16)
-    pcf = V(v.tensor_tensor(T.pcf[:, 0:1], T.c16[:, 0:1], T.c3[:, 0:1], A.add))
-    need("v", pcf, i2)
-    permo = V(v.tensor_scalar(T.permo[:, :], T.i2[:, :], T.pcf[:, 0:1], None, A.add))
+    act(T.maskb[:, :], T.maskf[:, :])
+    mb = act(T.blkb[:, :], T.blkf[:, :])
+    dlt = dma("s", T.snd3[:, :, :], T.ltb[:, :], "dlt", ltb)
+    dow3 = dma("s", T.land3[me, :, :], T.ltb[16 * me:16 * me + 16, :], "dow3")
+    need("g", dlt)
+    a3 = send(T.snd3, T.land3, "a3")
 
     need("y", a1, own, mpo)
     dst = dma("y", T.c0[:, :], T.land1[:, 64:80, :], "dst")
@@ -205,6 +191,9 @@ def rank_program(g, core, T, topo):
     for b in range(4):
         dpa = dma("y", T.poolw[16 * b:16 * b + 8, :], T.land1[:, 0:64, :], "dpa")
         dpb = dma("s", T.poolw[16 * b + 64:16 * b + 72, :], T.land1[:, 0:64, :], "dpb")
+    need("s", se)
+    act(T.lw[:, 0:1024], T.selw[:, :])
+    lwf = act(T.lw[:, 1024:2048], T.selw[:, :])
     need("y", a2, mwa)
     dwa = dma("y", T.wina[0:128:16, :], T.land2[:, :, :], "dwa")
     for q in range(16):
@@ -212,9 +201,10 @@ def rank_program(g, core, T, topo):
     dlw = dma("y", T.lw[0:128:16, :], T.land3[:, :, :], "dlw", a3, dow3, lwf)
 
     need("v", dst)
-    x = V(v.tensor_scalar(T.x[:, :], T.c0[:, :], float(KX), None, A.add))
+    ts(T.h2[:, :], T.c0[:, :], 2.0 ** -11, 2047.500244140625, A.mult, A.add)
+    sl = ts(T.sl[:, :], T.c0[:, :], 2047, None, A.bitwise_and)
     need("v", dpa, dpb, offm, selm)
-    gby = V(v.tensor_tensor(T.gby[:, :], T.poolw[:, :].indirect(T.offm[:, :]), T.selm[:, :], A.mult))
+    gby = tt(T.gby[:, :], T.poolw[:, :].indirect(T.offm[:, :]), T.selm[:, :], A.mult)
 
     segc = {}
 
@@ -225,27 +215,23 @@ def rank_program(g, core, T, topo):
             need("t", segc[b - 5])
         p = P(te.matmul(ps[:, :], T.selw[:, 128 * b:128 * b + 128], T.gby[:, :], True, True))
         need("s", p)
-        segc[b] = S(ac.activation(T.bw[:, 1 + 512 * b:513 + 512 * b], ps[:, :], F.Copy))
+        segc[b] = act(T.bw[:, 1 + 512 * b:513 + 512 * b], ps[:, :])
 
     offs = {}
 
     def letters(s):
         need("s", offs[s], dlw, permo)
         lg = T.lg[:, 128 * s:128 * s + 128]
-        t = S(ac.activation(lg, T.lw[:, :].indirect(T.off[:, 8 * s:8 * s + 8]), F.Copy))
-        need("s", t)
-        lg = T.lg[:, 128 * s:128 * s + 128]
-        return S(ac.activation(T.outs[:, 128 * s:128 * s + 128], lg.indirect(T.permo[:, :]), F.Copy))
+        need("s", act(lg, T.lw[:, :].indirect(T.off[:, 8 * s:8 * s + 8])))
+        return act(T.outs[:, 128 * s:128 * s + 128], lg.indirect(T.permo[:, :]))
 
     segment(0)
     segment(1)
-    prev = None
+    prev = offm
     outs = None
     for s in range(4):
         c = 8 * s
-        need("v", x)
-        t = V(v.tensor_scalar(T.sl[:, :], T.x[:, :], 2047, None, A.bitwise_and))
-        need("v", t)
+        need("v", sl)
         offs[s] = V(v.tensor_copy(T.off[:, c:c + 8], T.sl[:, :]))
         need("v", offs[s])
         if s == 0:
@@ -253,58 +239,69 @@ def rank_program(g, core, T, topo):
             t = V(v.tensor_copy(T.g0[:, :], T.wina[:, :].indirect(T.off[:, c:c + 8])))
             need("t", t, sg, plo, selm)
             t = P(te.matmul(T.psr[:, 0:128], T.sgf[:, :], T.g0[:, :], True, True))
-            h2 = V(v.tensor_scalar(T.h2[:, :], T.x[:, :], 2.0 ** -11, 0.500244140625, A.mult, A.add))
             need("v", t, mf)
-            gm = V(v.tensor_tensor(T.gm[:, :], T.psr[:, 0:128], T.maskf[:, :], A.mult))
+            gm = tt(T.gm[:, :], T.psr[:, 0:128], T.maskf[:, :], A.mult)
         else:
             need("v", dw)
-            gm = V(v.tensor_tensor(T.gm[:, :], T.win[:, :].indirect(T.off[:, c:c + 8]), T.maskf[:, :], A.mult))
-            h2 = V(v.tensor_scalar(T.h2[:, :], T.x[:, :], 2.0 ** -11, 0.500244140625, A.mult, A.add))
-        need("v", gm, h2, bf)
+            gm = tt(T.gm[:, :], T.win[:, :].indirect(T.off[:, c:c + 8]), T.maskf[:, :], A.mult)
+        need("v", gm, bf)
         e = V(v.tensor_tensor_scan(T.sc[:, :], T.blkf[:, :], T.gm[:, :], 0.0, A.mult, A.add))
         need("v", e)
         E = T.sc[:, 15:128:16]
-        f2 = V(v.tensor_scalar(T.f2[:, :], E, 2.0 ** -11, -2047.499755859375, A.mult, A.add))
-        u = V(v.tensor_tensor(T.u[:, :], T.x[:, :], E, A.subtract))
-        need("v", u)
-        pr = V(v.tensor_tensor(T.pr[:, :], T.f2[:, :], T.h2[:, :], A.mult))
-        need("v", pr)
-        xp = V(v.tensor_tensor(T.xp[:, :], T.pr[:, :], T.u[:, :], A.add))
-        need("v", xp)
-        w = V(v.tensor_scalar(T.w[:, :], T.xp[:, :], 4096.0, None, A.is_lt))
-        need("v", w, zer)
+        f3 = ts(T.f3[:, :], E, 2.0 ** -11, 0.500244140625, A.mult, A.add)
+        u = tt(T.u[:, :], T.sl[:, :], E, A.subtract)
+        need("v", f3)
+        pr = tt(T.pr[:, :], T.f3[:, :], T.h2[:, :], A.mult)
+        need("v", u, pr)
+        xq = tt(T.xq[:, :], T.pr[:, :], T.u[:, :], A.add)
+        need("t", prev, con)
+        te.matmul(T.psz[:, 0:8], T.ones[:, :], T.n64[:, :], True, False)
+        if s > 0:
+            te.matmul(T.psb[:, 0:1], T.ut[:, :], T.pp[:, c - 1:c], True, False)
+        need("v", xq)
+        w = ts(T.w[:, :], T.xq[:, :], 6144.0, None, A.is_lt)
+        n = ts(T.n[:, :], T.xq[:, :], -2048.0, 255.0, A.add, A.mult)
+        need("v", w)
         ini = 0.0 if s == 0 else T.pp[:, c - 1:c]
         pp = V(v.tensor_tensor_scan(T.pp[:, c:c + 8], T.w[:, :], T.zer[:, :], ini, A.add, A.max))
-        if s > 0:
-            need("t", prev, utm)
-            te.matmul(T.psb[:, 0:1], T.ut[:, :], T.pp[:, c - 1:c], True, False)
-        need("t", pp, ltm)
-        base = P(te.matmul(T.psb[:, 0:1], T.lt[:, :], T.pp[:, c + 7:c + 8], s == 0, True))
-        nr = V(v.tensor_scalar(T.nr[:, :], T.xp[:, :], 4096.0, -8192.0, A.is_ge, A.mult))
-        m = V(v.tensor_tensor(T.m[:, :], T.w[:, :], T.xp[:, :], A.mult))
-        need("v", pp, m)
-        pm = V(v.tensor_tensor(T.pm[:, :], T.pp[:, c:c + 8], T.nr[:, :], A.add))
-        n = V(v.tensor_scalar(T.n[:, :], T.m[:, :], 255.0, float(KX if s < 3 else 0), A.mult, A.add))
-        need("v", pm, n)
-        y = V(v.tensor_tensor(T.y[:, :], T.n[:, :], T.xp[:, :], A.add))
+        need("t", w)
+        te.matmul(T.psz[:, 0:8], T.i8k[:, :], T.w[:, :], False, False)
+        need("t", pp)
+        te.matmul(T.psb[:, 0:1], T.lt[:, :], T.pp[:, c + 7:c + 8], s == 0, True)
+        base = P(te.matmul(T.psz[:, 0:8], T.idn[:, :], T.pp[:, c:c + 8], False, True))
+        need("v", n)
+        m = tt(T.m[:, :], T.n[:, :], T.w[:, :], A.mult)
+        need("v", m)
+        y = tt(T.y[:, :], T.m[:, :], T.xq[:, :], A.add)
+        if s == 3:
+            need("v", y)
+            y = ts(T.yt[:, :], T.y[:, :], -2048.0, None, A.add)
         need("v", base)
-        prev = V(v.tensor_scalar(T.off2[:, c:c + 8], T.pm[:, :], T.psb[:, 0:1], 0.0, A.add, A.max))
-        need("v", prev, mb, bb_, bw0, segc[2 * s + 1])
-        t = V(v.tensor_tensor(T.gb[:, :], T.bw[:, 0:1025 + 1024 * s].indirect(T.off2[:, c:c + 8]), T.maskb[:, :], A.mult))
+        prev = ts(T.off2[:, c:c + 8], T.psz[:, 0:8], T.psb[:, 0:1], 0.0, A.add, A.max)
+        need("v", prev, mb, con, segc[2 * s + 1])
+        t = tt(T.gb[:, :], T.bw[:, 0:1025 + 1024 * s].indirect(T.off2[:, c:c + 8]), T.maskb[:, :], A.mult)
+        if s < 3:
+            need("v", y)
+            ts(T.h2[:, :], T.y[:, :], 2.0 ** -11, 2046.500244140625, A.mult, A.add)
+            ylo = ts(T.ylo[:, :], T.y[:, :], 2047, None, A.bitwise_and)
         need("v", t)
         t = V(v.tensor_tensor_scan(T.sb[:, :], T.blkb[:, :], T.gb[:, :], 0.0, A.mult, A.add))
         need("v", t, y)
-        x = V(v.tensor_tensor(T.x[:, :] if s < 3 else T.xl[:, :], T.y[:, :], T.sb[:, 15:128:16], A.add))
         if s < 3:
+            sl = tt(T.sl[:, :], T.ylo[:, :], T.sb[:, 15:128:16], A.add)
             segment(2 * s + 2)
             segment(2 * s + 3)
-        outs = letters(s)
+        else:
+            xl = tt(T.xl[:, :], T.yt[:, :], T.sb[:, 15:128:16], A.add)
+        if s > 0:
+            letters(s - 1)
+    outs = letters(3)
 
     dsy = dma("s", T.snd4[:, :, :], T.outs[0:128:16, :], "dsy", outs)
     dow4 = dma("s", T.land4[me, :, :], T.outs[16 * me:16 * me + 1, :], "dow4")
     need("g", dsy)
     a4 = send(T.snd4, T.land4, "a4")
-    dla = dma("y", T.snd5[:, :, :], T.xl[:, :], "dla", x)
+    dla = dma("y", T.snd5[:, :, :], T.xl[:, :], "dla", xl)
     dow5 = dma("y", T.land5[me, :, :], T.xl[16 * me:16 * me + 16, :], "dow5")
     need("g", dla)
     a5 = send(T.snd5, T.land5, "a5")

@@ -3,24 +3,24 @@ from concourse.mybir import AluOpType as A, ActivationFunctionType as F
 
 I32, U16, F32, B16 = "int32", "uint16", "float32", "bfloat16"
 SCRATCH = {}
-for _i, _w, _t in ((1, 8, I32), (2, 16, I32), (3, 16, B16), (4, 4, F32), (5, 1, F32)):
+for _i, _w, _t in ((1, 24, I32), (3, 16, B16), (4, 4, F32), (5, 1, F32)):
     SCRATCH["snd%d" % _i] = SCRATCH["land%d" % _i] = ("dram", [8, 128, _w], _t)
 for _t, _l in (
-        (I32, "ia 128 ic 128 ij 128 ip 8 i2 8 cq 8 c7 8 c3 8 sgi 128 i32i 32 ind4i 4 pl 32 zz 32 zh 32 loi 32 poolw 512"
-              " wina 2048 win 2048 lti 128 c0 8 f3 8 h2 8 y 8 ylo 8 sl 8"),
+        (I32, "ia 128 ic 128 ij 128 ip 8 i2 8 i4 4 i3o 32 cq 8 c7 8 c3 8 sgi 128 i32i 32 ind4i 4 pl 32 zz 32 zh 32 zq 32"
+              " zm 32 zc 32 loi 32 poolw 648 wina 2064 win 2064 lti 128 c0 8 f3 8 h2 8 y 8 ylo 8 sl 8"),
         (U16, "permo 8 offm 32 off 32 off2 32"),
-        (F32, "qf 8 p15 8 c16 8 pcf 8 maskf 128 blkf 128 sgf 128 i32f 32 ind4 4 lz 256 g0 128 gm 128 sc 128 u 8 pr 8 xq 8"
-              " m 8 n 8 yt 8 xl 8 lg 512 outs 512"),
+        (F32, "qf 8 p15 8 c16 8 pcf 8 maskf 128 blkf 128 sgf 128 i32f 32 ind4 4 lz 256 g0 128 gm 128 sc 128 u 8 u4 8 pr 8"
+              " xq 8 m 8 n 8 yt 8 xl 8 lg 512 outs 512"),
         (B16, "maskb 128 blkb 128 lt 128 ut 128 e8 128 ones 128 idn 128 i8k 128 n64 8 selw 1024 zer 8 lob 32 selm 512"
-              " gby 512 bw 4112 ltb 128 lw 2048 w 8 pp 32 sb 128 gb 128")):
+              " gby 512 bw 4112 ltb 128 lw 2064 w 8 pp 32 sb 128 gb 128")):
     _l = _l.split()
     for _i in range(0, len(_l), 2):
         SCRATCH[_l[_i]] = ("sbuf", [128, int(_l[_i + 1])], _t)
 SCRATCH["lor"] = ("sbuf", [8, 512], B16)
 for _i in ("ps0", "ps1", "ps2", "ps3", "ps4", "psr", "psz", "psb"):
     SCRATCH[_i] = ("psum", [128, 512], F32)
-SEMAPHORES = ["gi", "v", "t", "s", "ls", "a1", "a2", "a3", "a4", "a5",
-              "l1", "l2", "own", "lpl", "lzz", "llt", "dlo", "dlt", "dow3", "dst", "dpa", "dpb", "dwa", "dw", "dlw",
+SEMAPHORES = ["gi", "v", "t", "s", "ls", "a1", "a3", "a4", "a5",
+              "l1", "own", "lpl", "lzz", "llt", "dlo", "dlt", "dow3", "dst", "dpa", "dpb", "dwa", "dw", "dlw",
               "dsy", "dow4", "dla", "dow5", "fsy", "fla"]
 
 
@@ -64,6 +64,9 @@ def rank_program(g, core, T, topo):
     def tt(out, a, b, op):
         return V(v.tensor_tensor(out, a, b, op))
 
+    def fill(ap, x):
+        return V(v.memset(ap, x))
+
     def act(out, in_, *sc):
         return S(ac.activation(out, in_, F.Copy, *sc))
 
@@ -90,88 +93,101 @@ def rank_program(g, core, T, topo):
         cnt[arr] = len(others)
         return (arr, len(others))
 
-    dma("y", T.snd1[:, 0:64, :], T.stock[:, :], "l1")
-    l2 = dma("s", T.snd2[:, :, :], T.models[:, :], "l2")
-    dma("y", T.snd1[:, 64:80, :], T.states[:, :], "l1")
-    l1 = dma("y", T.snd1[:, 80:128, :], T.stock[:, 0:384], "l1")
-    lpl = dma("s", T.pl[:, :], T.places[me, :], "lpl")
-    dma("s", T.zz[:, 0:16], T.places[me, 0:2048], "lzz")
-    lzz = dma("s", T.zz[:, 16:32], T.places[me, 2048:4096], "lzz")
-    dma("y", T.land1[me, 0:64, :], T.stock[me, :], "own")
-    dma("y", T.land1[me, 64:80, :], T.states[me, :], "own")
-    own = dma("y", T.land2[me, :, :], T.models[me, :], "own")
-    llt = dma("s", T.lti[:, :], T.letters[:, :], "llt")
+    dma("y", T.snd1[:, 27:112, :], T.models[:, 8:2048], "l1")
+    dma("s", T.snd1[:, 0:16, 8:24], T.stock[:, 0:256], "l1")
+    dma("y", T.snd1[:, 26, 16:24], T.models[:, 0:8], "l1")
+    dma("s", T.snd1[:, 0:16, 0:8], T.states[:, :], "l1")
+    dma("y", T.snd1[:, 26, 0:16], T.stock[:, 496:512], "l1")
+    dma("s", T.snd1[:, 16:26, :], T.stock[:, 256:496], "l1")
+    l1 = dma("y", T.snd1[:, 112:128, :], T.models[:, 0:384], "l1")
+    lpl = dma("y", T.pl[:, :], T.places[me, :], "lpl")
+    for s in range(4):
+        for h in range(2):
+            t = 1024 * s + 512 * h
+            lzz = dma("s", T.zz[32 * s:32 * s + 32, 16 * h:16 * h + 16], T.places[me, t:t + 512], "lzz")
+    llt = dma("y", T.lti[:, :], T.letters[:, :], "llt")
+    own = dma("y", T.land1[me, :, :], T.snd1[me, :, :], "own", l1)
 
     ic = did(g.iota(T.ic[:, :], [[-16, 8], [0, 16]], 0, 1), "gi")
     ip = did(g.iota(T.ip[:, 0:1], [[0, 1]], 0, 1), "gi")
-    ia = did(g.iota(T.ia[:, :], [[-1, 128]], 0, 1), "gi")
+    i4 = did(g.iota(T.i4[:, :], [[-8, 4]], 0, 1), "gi")
+    i3o = did(g.iota(T.i3o[:, :], [[-32, 4], [-1, 8]], 128, 1), "gi")
     ij = did(g.iota(T.ij[:, :], [[0, 8], [1, 16]], 0, 0), "gi")
+    ia = did(g.iota(T.ia[:, :], [[-1, 128]], 0, 1), "gi")
     i2 = did(g.iota(T.i2[:, :], [[2, 8]], 0, 0), "gi")
     need("g", l1)
     a1 = send(T.snd1, T.land1, "a1")
-    need("g", l2)
-    a2 = send(T.snd2, T.land2, "a2")
 
-    ones = V(v.memset(T.ones[:, :], 1.0))
-    mpo = V(v.memset(T.poolw[:, :], 0))
+    ones = fill(T.ones[:, :], 1.0)
+    fill(T.wina[:, 0:256], 0)
     need("v", ic, ip)
     sgi = ts(T.sgi[:, :], T.ic[:, :], 4, None, A.arith_shift_right)
     p15 = ts(T.p15[:, 0:1], T.ip[:, 0:1], 15.0, None, A.mult)
     cq = ts(T.cq[:, 0:1], T.ip[:, 0:1], 15, None, A.bitwise_and)
-    n4i = ts(T.ind4i[:, :], T.ic[:, 0:128:32], 5, None, A.arith_shift_right)
-    need("v", n4i)
+    mpo = fill(T.poolw[:, :], 0)
+    need("v", cq)
     sg = ts(T.sgf[:, :], T.sgi[:, :], 0.0, None, A.is_equal)
     e8 = ts(T.e8[:, :], T.ic[:, :], T.p15[:, 0:1], 0.0, A.add, A.is_equal)
     qf = V(v.tensor_copy(T.qf[:, 0:1], T.cq[:, 0:1]))
+    need("v", i4, i3o)
+    n4i = ts(T.ind4i[:, :], T.i4[:, :], 31, 3, A.bitwise_and, A.arith_shift_right)
+    i3i = ts(T.i32i[:, :], T.i3o[:, :], 231, None, A.bitwise_and)
+    fill(T.wina[:, 256:1152], 0)
+    need("v", i3i)
     n4 = ts(T.ind4[:, :], T.ind4i[:, :], 0.0, None, A.is_equal)
-    need("v", ia)
-    i3i = ts(T.i32i[:, :], T.ia[:, 0:32], 31, None, A.bitwise_and)
-    mwa = V(v.memset(T.wina[:, :], 0))
-    i3 = ts(T.i32f[:, :], T.i32i[:, :], 0.0, None, A.is_equal) if not need("v", mwa) else None
-    lz0 = V(v.memset(T.lz[:, :], 0.0))
+    i3 = ts(T.i32f[:, :], T.i32i[:, :], 128.0, None, A.is_equal)
     need("v", lpl)
     loi = ts(T.loi[:, :], T.pl[:, :], 7, None, A.bitwise_and)
     need("v", lzz)
     zh = ts(T.zh[:, :], T.zz[:, :], 3, None, A.arith_shift_right)
-    need("v", zh)
+    zq = ts(T.zq[:, :], T.zz[:, :], 7, None, A.arith_shift_right)
+    fill(T.wina[:, 1152:1600], 0)
+    need("v", zq)
     lob = V(v.tensor_copy(T.lob[:, :], T.loi[:, :]))
+    zm = ts(T.zm[:, :], T.zq[:, :], 15.0, 8.0, A.min, A.mult)
+    mwa = fill(T.wina[:, 1600:2064], 0)
+    need("v", zm)
+    zc = tt(T.zc[:, :], T.zh[:, :], T.zm[:, :], A.add)
+    lz0 = fill(T.lz[:, :], 0.0)
+    ts(T.c7[:, 0:1], T.ip[:, 0:1], 7, None, A.bitwise_and)
+    c3 = ts(T.c3[:, 0:1], T.ip[:, 0:1], 3, 1, A.arith_shift_right, A.bitwise_and)
+    need("v", lz0, zc)
     lz = None
     for b in range(8):
         h, bb = b // 4, b % 4
         c = 128 * h + 16 * b
-        lz = ts(T.lz[:, c:c + 16], T.zh[:, 16 * h:16 * h + 16], T.ind4[:, bb:bb + 1], None, A.mult)
+        lz = ts(T.lz[:, c:c + 16], T.zc[:, 16 * h:16 * h + 16], T.ind4[:, bb:bb + 1], None, A.mult)
     need("v", ij)
     mf = ts(T.maskf[:, :], T.ij[:, :], T.qf[:, 0:1], None, A.is_equal)
     bf = ts(T.blkf[:, :], T.ij[:, :], 0.0, None, A.is_gt)
     need("v", llt)
     ltb = V(v.tensor_copy(T.ltb[:, :], T.lti[:, :]))
+    need("v", c3)
+    c16 = ts(T.c16[:, 0:1], T.c7[:, 0:1], 16.0, None, A.mult)
+    need("v", ia)
     ts(T.lt[:, :], T.ia[:, :], 0.0, None, A.is_lt)
     ts(T.ut[:, :], T.ia[:, :], 0.0, None, A.is_gt)
+    need("v", c16)
+    pcf = tt(T.pcf[:, 0:1], T.c16[:, 0:1], T.c3[:, 0:1], A.add)
     ts(T.idn[:, :], T.ia[:, :], 0.0, None, A.is_equal)
     ts(T.i8k[:, :], T.ia[:, :], 0.0, 8192.0, A.is_equal, A.mult)
-    V(v.memset(T.zer[:, :], 0.0))
-    V(v.memset(T.n64[:, :], -64.0))
-    con = V(v.memset(T.bw[:, 0:1], 0.0))
+    fill(T.zer[:, :], 0.0)
+    fill(T.n64[:, :], -64.0)
+    con = fill(T.bw[:, 0:1], 0.0)
+    need("v", pcf, i2)
+    permo = ts(T.permo[:, :], T.i2[:, :], T.pcf[:, 0:1], None, A.add)
 
     need("t", lz, i3)
     te.matmul(T.psz[:, 0:32], T.lz[:, 0:128], T.i32f[:, :], True, False)
     pz = P(te.matmul(T.psz[:, 0:32], T.lz[:, 128:256], T.i32f[:, :], False, True))
-    dlo = dma("y", T.lor[:, :], T.lob[:, :], "dlo", lob)
+    for s in range(4):
+        dlo = dma("y", T.lor[:, 128 * s:128 * s + 128], T.lob[32 * s:32 * s + 32, :], "dlo", lob)
     need("t", dlo, e8)
-    plo = P(te.matmul(T.psr[:, :], T.e8[0:8, :], T.lor[:, :], True, True))
-
+    plo = P(te.matmul(T.ps4[:, :], T.e8[0:8, :], T.lor[:, :], True, True))
     need("v", pz)
-    offm = V(v.tensor_copy(T.offm[:, :], T.psz[:, 0:32]))
-    ts(T.c7[:, 0:1], T.ip[:, 0:1], 7, None, A.bitwise_and)
-    c3 = ts(T.c3[:, 0:1], T.ip[:, 0:1], 3, 1, A.arith_shift_right, A.bitwise_and)
-    need("v", c3)
-    c16 = ts(T.c16[:, 0:1], T.c7[:, 0:1], 16.0, None, A.mult)
-    need("v", c16)
-    pcf = tt(T.pcf[:, 0:1], T.c16[:, 0:1], T.c3[:, 0:1], A.add)
-    need("v", pcf, i2)
-    permo = ts(T.permo[:, :], T.i2[:, :], T.pcf[:, 0:1], None, A.add)
+    offm = ts(T.offm[:, :], T.psz[:, 0:32], 8.0, None, A.add)
     need("v", plo)
-    selm = ts(T.selm[:, :], T.psr[:, :], T.qf[:, 0:1], None, A.is_equal)
+    selm = ts(T.selm[:, :], T.ps4[:, :], T.qf[:, 0:1], None, A.is_equal)
 
     need("s", ones, sg)
     se = None
@@ -185,39 +201,45 @@ def rank_program(g, core, T, topo):
     need("g", dlt)
     a3 = send(T.snd3, T.land3, "a3")
 
-    need("y", a1, own, mpo)
-    dst = dma("y", T.c0[:, :], T.land1[:, 64:80, :], "dst")
+    need("y", a1, own, mpo, mwa)
     need("s", a1, own, mpo)
+    dst = dma("y", T.c0[:, :], T.land1[:, 0:16, 0:8], "dst")
+    dwa = dma("y", T.wina[0:128:16, :], T.land1[:, 26:112, :], "dwa")
     for b in range(4):
-        dpa = dma("y", T.poolw[16 * b:16 * b + 8, :], T.land1[:, 0:64, :], "dpa")
-        dpb = dma("s", T.poolw[16 * b + 64:16 * b + 72, :], T.land1[:, 0:64, :], "dpb")
+        dpb = dma("s", T.poolw[16 * b:16 * b + 8, :], T.land1[:, 0:27, :], "dpb")
+        dpa = dma("y", T.poolw[16 * b + 64:16 * b + 72, :], T.land1[:, 0:27, :], "dpa")
+    for q in range(16):
+        dw = dma("y", T.win[q:128:16, :], T.land1[:, 26:112, :], "dw")
     need("s", se)
     act(T.lw[:, 0:1024], T.selw[:, :])
+    act(T.lw[:, 2048:2064], T.selw[:, 0:16])
     lwf = act(T.lw[:, 1024:2048], T.selw[:, :])
-    need("y", a2, mwa)
-    dwa = dma("y", T.wina[0:128:16, :], T.land2[:, :, :], "dwa")
-    for q in range(16):
-        dw = dma("y", T.win[q:128:16, :], T.land2[:, :, :], "dw")
-    dlw = dma("y", T.lw[0:128:16, :], T.land3[:, :, :], "dlw", a3, dow3, lwf)
+    dlw = dma("y", T.lw[0:128:16, 16:2064], T.land3[:, :, :], "dlw", a3, dow3, lwf)
 
     need("v", dst)
-    ts(T.h2[:, :], T.c0[:, :], 2.0 ** -11, 2047.500244140625, A.mult, A.add)
     sl = ts(T.sl[:, :], T.c0[:, :], 2047, None, A.bitwise_and)
-    need("v", dpa, dpb, offm, selm)
-    gby = tt(T.gby[:, :], T.poolw[:, :].indirect(T.offm[:, :]), T.selm[:, :], A.mult)
+    h2 = ts(T.h2[:, :], T.c0[:, :], 2.0 ** -11, 2047.500244140625, A.mult, A.add)
 
-    segc = {}
+    gby, segc, offs = {}, {}, {}
 
-    def segment(b):
-        ps = T["ps%d" % (b % 5)]
-        need("t", gby, se)
-        if b >= 5:
-            need("t", segc[b - 5])
-        p = P(te.matmul(ps[:, :], T.selw[:, 128 * b:128 * b + 128], T.gby[:, :], True, True))
+    def gather(s0, s1):
+        r = tt(T.gby[:, 128 * s0:128 * s1], T.poolw[:, :].indirect(T.offm[:, 8 * s0:8 * s1]),
+               T.selm[:, 128 * s0:128 * s1], A.mult)
+        for s in range(s0, s1):
+            gby[s] = r
+
+    def segment(i):
+        ps = T["ps%d" % (i % 5)]
+        s, p = i // 2, None
+        need("t", gby[s], se)
+        if i >= 5:
+            need("t", segc[i - 5])
+        for k in range(4):
+            b = 4 * (i % 2) + k
+            p = P(te.matmul(ps[:, 128 * k:128 * k + 128], T.selw[:, 128 * b:128 * b + 128],
+                            T.gby[:, 128 * s:128 * s + 128], True, True))
         need("s", p)
-        segc[b] = act(T.bw[:, 1 + 512 * b:513 + 512 * b], ps[:, :])
-
-    offs = {}
+        segc[i] = act(T.bw[:, 1 + 512 * i:513 + 512 * i], ps[:, :])
 
     def letters(s):
         need("s", offs[s], dlw, permo)
@@ -225,42 +247,45 @@ def rank_program(g, core, T, topo):
         need("s", act(lg, T.lw[:, :].indirect(T.off[:, 8 * s:8 * s + 8])))
         return act(T.outs[:, 128 * s:128 * s + 128], lg.indirect(T.permo[:, :]))
 
-    segment(0)
-    segment(1)
     prev = offm
-    outs = None
     for s in range(4):
         c = 8 * s
         need("v", sl)
-        offs[s] = V(v.tensor_copy(T.off[:, c:c + 8], T.sl[:, :]))
+        offs[s] = ts(T.off[:, c:c + 8], T.sl[:, :], 16.0, None, A.add)
         need("v", offs[s])
         if s == 0:
             need("v", dwa)
             t = V(v.tensor_copy(T.g0[:, :], T.wina[:, :].indirect(T.off[:, c:c + 8])))
-            need("t", t, sg, plo, selm)
+            need("t", t, sg)
             t = P(te.matmul(T.psr[:, 0:128], T.sgf[:, :], T.g0[:, :], True, True))
+            need("v", dpa, dpb, offm, selm)
+            gather(0, 1)
+            gather(1, 3)
+            segment(0)
+            segment(1)
             need("v", t, mf)
             gm = tt(T.gm[:, :], T.psr[:, 0:128], T.maskf[:, :], A.mult)
         else:
             need("v", dw)
             gm = tt(T.gm[:, :], T.win[:, :].indirect(T.off[:, c:c + 8]), T.maskf[:, :], A.mult)
+            h2 = ts(T.h2[:, :], T.y[:, :], 2.0 ** -11, 2046.500244140625, A.mult, A.add)
         need("v", gm, bf)
         e = V(v.tensor_tensor_scan(T.sc[:, :], T.blkf[:, :], T.gm[:, :], 0.0, A.mult, A.add))
         need("v", e)
         E = T.sc[:, 15:128:16]
         f3 = ts(T.f3[:, :], E, 2.0 ** -11, 0.500244140625, A.mult, A.add)
         u = tt(T.u[:, :], T.sl[:, :], E, A.subtract)
-        need("v", f3)
+        need("v", f3, h2)
         pr = tt(T.pr[:, :], T.f3[:, :], T.h2[:, :], A.mult)
-        need("v", u, pr)
-        xq = tt(T.xq[:, :], T.pr[:, :], T.u[:, :], A.add)
+        need("v", u)
+        u4 = ts(T.u4[:, :], T.u[:, :], -1.0, 6144.0, A.mult, A.add)
         need("t", prev, con)
         te.matmul(T.psz[:, 0:8], T.ones[:, :], T.n64[:, :], True, False)
         if s > 0:
             te.matmul(T.psb[:, 0:1], T.ut[:, :], T.pp[:, c - 1:c], True, False)
-        need("v", xq)
-        w = ts(T.w[:, :], T.xq[:, :], 6144.0, None, A.is_lt)
-        n = ts(T.n[:, :], T.xq[:, :], -2048.0, 255.0, A.add, A.mult)
+        need("v", pr, u4)
+        w = tt(T.w[:, :], T.pr[:, :], T.u4[:, :], A.is_lt)
+        xq = tt(T.xq[:, :], T.pr[:, :], T.u[:, :], A.add)
         need("v", w)
         ini = 0.0 if s == 0 else T.pp[:, c - 1:c]
         pp = V(v.tensor_tensor_scan(T.pp[:, c:c + 8], T.w[:, :], T.zer[:, :], ini, A.add, A.max))
@@ -269,24 +294,26 @@ def rank_program(g, core, T, topo):
         need("t", pp)
         te.matmul(T.psb[:, 0:1], T.lt[:, :], T.pp[:, c + 7:c + 8], s == 0, True)
         base = P(te.matmul(T.psz[:, 0:8], T.idn[:, :], T.pp[:, c:c + 8], False, True))
+        need("v", xq)
+        n = ts(T.n[:, :], T.xq[:, :], -2048.0, 255.0, A.add, A.mult)
+        if s == 0:
+            gather(3, 4)
         need("v", n)
         m = tt(T.m[:, :], T.n[:, :], T.w[:, :], A.mult)
-        need("v", m)
-        y = tt(T.y[:, :], T.m[:, :], T.xq[:, :], A.add)
-        if s == 3:
-            need("v", y)
-            y = ts(T.yt[:, :], T.y[:, :], -2048.0, None, A.add)
         need("v", base)
         prev = ts(T.off2[:, c:c + 8], T.psz[:, 0:8], T.psb[:, 0:1], 0.0, A.add, A.max)
+        need("v", m)
+        y = tt(T.y[:, :], T.m[:, :], T.xq[:, :], A.add)
         need("v", prev, mb, con, segc[2 * s + 1])
         t = tt(T.gb[:, :], T.bw[:, 0:1025 + 1024 * s].indirect(T.off2[:, c:c + 8]), T.maskb[:, :], A.mult)
+        need("v", y)
         if s < 3:
-            need("v", y)
-            ts(T.h2[:, :], T.y[:, :], 2.0 ** -11, 2046.500244140625, A.mult, A.add)
-            ylo = ts(T.ylo[:, :], T.y[:, :], 2047, None, A.bitwise_and)
+            y2 = ts(T.ylo[:, :], T.y[:, :], 2047, None, A.bitwise_and)
+        else:
+            y2 = ts(T.yt[:, :], T.y[:, :], -2048.0, None, A.add)
         need("v", t)
         t = V(v.tensor_tensor_scan(T.sb[:, :], T.blkb[:, :], T.gb[:, :], 0.0, A.mult, A.add))
-        need("v", t, y)
+        need("v", t, y2)
         if s < 3:
             sl = tt(T.sl[:, :], T.ylo[:, :], T.sb[:, 15:128:16], A.add)
             segment(2 * s + 2)

@@ -3,25 +3,27 @@ from concourse.mybir import AluOpType as A, ActivationFunctionType as F
 
 I32, U16, F32, B16 = "int32", "uint16", "float32", "bfloat16"
 SCRATCH = {}
-for _i, _w, _t in ((1, 24, I32), (3, 16, B16), (4, 4, F32), (5, 1, F32)):
+for _i, _w, _t in ((0, 8, I32), (1, 16, I32), (2, 16, B16), (3, 16, B16), (4, 4, F32), (5, 1, F32)):
     SCRATCH["snd%d" % _i] = SCRATCH["land%d" % _i] = ("dram", [8, 128, _w], _t)
 for _t, _l in (
-        (I32, "ia 128 ic 128 ij 128 ip 8 i2 8 i4 4 i3o 32 cq 8 c7 8 c3 8 sgi 128 i32i 32 ind4i 4 pl 32 zz 32 zh 32 zq 32"
-              " zm 32 zc 32 loi 32 poolw 648 wina 2064 win 2064 lti 128 c0 8 f3 8 h2 8 y 8 ylo 8 sl 8"),
-        (U16, "permo 8 offm 32 off 32 off2 32"),
-        (F32, "qf 8 p15 8 c16 8 pcf 8 maskf 128 blkf 128 sgf 128 i32f 32 ind4 4 lz 256 g0 128 gm 128 sc 128 u 8 u4 8 pr 8"
-              " xq 8 m 8 n 8 yt 8 xl 8 lg 512 outs 512"),
-        (B16, "maskb 128 blkb 128 lt 128 ut 128 e8 128 ones 128 idn 128 i8k 128 n64 8 selw 1024 zer 8 lob 32 selm 512"
-              " gby 512 bw 4112 ltb 128 lw 2064 w 8 pp 32 sb 128 gb 128")):
+        (I32, "ic 128 ij 128 is1 128 ip 8 i2 8 i1 8 i4 4 i3o 32 cq 8 c7 8 c3 8 ch 8 c1 8 c8 8 sgi 128 i32i 32"
+              " ind4i 4 pl 32 zz 32 zh 32 loi 32 lh 32 poolw 256 wq 128 win 2048 lti 128 c0 8 k 8 lo 8 f3 8 h2 8"
+              " y 8 ylo 8 sl 8 mt 128 mf 128 mc 128 mq 128 sa 128"),
+        (U16, "permo 8 clist 8 offm 32 off 32 off0 8 off2 32"),
+        (F32, "qf 8 qs 8 p15 8 c16 8 pcf 8 maskf 128 blkf 128 bmask 128 hxm 128 sgf 128 i32f 32 ind4 4 lz 256 selx 128 g0 128"
+              " gm 128 sc 128 slm 8 u 8 u4 8 pr 8 xq 8 g256 8 xl 8 lg 512 outs 512 sp 128 mff 128 mn 128 mr 128 mv 128"),
+        (B16, "blkb 128 lt 128 e8 128 ones 128 c255 128 n255 128 idn 128 nid 128 i128 8 selw 1024 sgb 128 km 128 zer 128"
+              " lob 32 selm 512 gby 512 bw 4112 ltb 128 lw 2048 thw 2048 qb 128 maskb 128 w 8 wm 128 pp 8 ppx 432 sb 128"
+              " gb 128")):
     _l = _l.split()
     for _i in range(0, len(_l), 2):
         SCRATCH[_l[_i]] = ("sbuf", [128, int(_l[_i + 1])], _t)
 SCRATCH["lor"] = ("sbuf", [8, 512], B16)
 for _i in ("ps0", "ps1", "ps2", "ps3", "ps4", "psr", "psz", "psb"):
     SCRATCH[_i] = ("psum", [128, 512], F32)
-SEMAPHORES = ["gi", "v", "t", "s", "ls", "a1", "a3", "a4", "a5",
-              "l1", "own", "lpl", "lzz", "llt", "dlo", "dlt", "dow3", "dst", "dpa", "dpb", "dwa", "dw", "dlw",
-              "dsy", "dow4", "dla", "dow5", "fsy", "fla"]
+SEMAPHORES = ["gi", "v", "t", "s", "ls", "a0", "a1", "a2", "a3", "a4", "a5",
+              "l0", "l1", "own0", "own1", "lmt", "lpl", "lzz", "llt", "dlo", "dth", "dlt", "dow2", "dow3", "dst", "dpa",
+              "dpb", "dwa", "dw", "dtw", "dlw", "dsy", "dow4", "dla", "dow5", "fsy", "fla"]
 
 
 def rank_program(g, core, T, topo):
@@ -64,6 +66,12 @@ def rank_program(g, core, T, topo):
     def tt(out, a, b, op):
         return V(v.tensor_tensor(out, a, b, op))
 
+    def scan(out, a, b, o1, o2):
+        return V(v.tensor_tensor_scan(out, a, b, 0.0, o1, o2))
+
+    def copy(out, in_):
+        return V(v.tensor_copy(out, in_))
+
     def fill(ap, x):
         return V(v.memset(ap, x))
 
@@ -93,134 +101,165 @@ def rank_program(g, core, T, topo):
         cnt[arr] = len(others)
         return (arr, len(others))
 
-    dma("y", T.snd1[:, 27:112, :], T.models[:, 8:2048], "l1")
-    dma("s", T.snd1[:, 0:16, 8:24], T.stock[:, 0:256], "l1")
-    dma("y", T.snd1[:, 26, 16:24], T.models[:, 0:8], "l1")
-    dma("s", T.snd1[:, 0:16, 0:8], T.states[:, :], "l1")
-    dma("y", T.snd1[:, 26, 0:16], T.stock[:, 496:512], "l1")
-    dma("s", T.snd1[:, 16:26, :], T.stock[:, 256:496], "l1")
-    l1 = dma("y", T.snd1[:, 112:128, :], T.models[:, 0:384], "l1")
+    dma("s", T.snd0[:, 0:16, :], T.states[:, :], "l0")
+    dma("y", T.snd0[:, 16:80, :], T.stock[:, :], "l0")
+    l0 = dma("s", T.snd0[:, 80:128, :], T.models[:, 0:384], "l0")
+    l1 = dma("y", T.snd1[:, :, :], T.models[:, :], "l1")
+    lmt = dma("y", T.mt[:, :], T.models[:, :], "lmt")
     lpl = dma("y", T.pl[:, :], T.places[me, :], "lpl")
     for s in range(4):
         for h in range(2):
             t = 1024 * s + 512 * h
             lzz = dma("s", T.zz[32 * s:32 * s + 32, 16 * h:16 * h + 16], T.places[me, t:t + 512], "lzz")
     llt = dma("y", T.lti[:, :], T.letters[:, :], "llt")
-    own = dma("y", T.land1[me, :, :], T.snd1[me, :, :], "own", l1)
+    dma("y", T.land0[me, 0:16, :], T.states[me, :], "own0")
+    own0 = dma("y", T.land0[me, 16:80, :], T.stock[me, :], "own0")
+    own1 = dma("y", T.land1[me, :, :], T.models[me, :], "own1")
 
-    ic = did(g.iota(T.ic[:, :], [[-16, 8], [0, 16]], 0, 1), "gi")
-    ip = did(g.iota(T.ip[:, 0:1], [[0, 1]], 0, 1), "gi")
-    i4 = did(g.iota(T.i4[:, :], [[-8, 4]], 0, 1), "gi")
-    i3o = did(g.iota(T.i3o[:, :], [[-32, 4], [-1, 8]], 128, 1), "gi")
-    ij = did(g.iota(T.ij[:, :], [[0, 8], [1, 16]], 0, 0), "gi")
-    ia = did(g.iota(T.ia[:, :], [[-1, 128]], 0, 1), "gi")
-    i2 = did(g.iota(T.i2[:, :], [[2, 8]], 0, 0), "gi")
+    def pattern(out, pat, base, mul):
+        return did(g.iota(out, pat, base, mul), "gi")
+
+    def choose(out, in_, step, op, mul, *toks):
+        need("g", *toks)
+        return did(g.affine_select(out, in_, [[step, 128]], op, 0.0, 0, mul), "gi")
+
+    ip = pattern(T.ip[:, 0:1], [[0, 1]], 0, 1)
+    ic = pattern(T.ic[:, :], [[-16, 8], [0, 16]], 0, 1)
+    is1 = pattern(T.is1[:, :], [[1, 128]], 0, 128)
+    ij = pattern(T.ij[:, :], [[0, 8], [1, 16]], 0, 0)
+    need("g", l0)
+    a0 = send(T.snd0, T.land0, "a0")
     need("g", l1)
     a1 = send(T.snd1, T.land1, "a1")
+    i4 = pattern(T.i4[:, :], [[-8, 4]], 0, 1)
+    i3o = pattern(T.i3o[:, :], [[-32, 4], [-1, 8]], 128, 1)
+    i1 = pattern(T.i1[:, :], [[1, 8]], 0, 0)
+    i2 = pattern(T.i2[:, :], [[2, 8]], 0, 0)
 
     ones = fill(T.ones[:, :], 1.0)
-    fill(T.wina[:, 0:256], 0)
-    need("v", ic, ip)
-    sgi = ts(T.sgi[:, :], T.ic[:, :], 4, None, A.arith_shift_right)
-    p15 = ts(T.p15[:, 0:1], T.ip[:, 0:1], 15.0, None, A.mult)
+    fill(T.c255[:, :], 255.0)
+    n255 = fill(T.n255[:, :], -255.0)
+    lt = choose(T.lt[:, :], T.ones[:, :], 1, A.is_gt, -1, ones)
+    lz0 = fill(T.lz[:, :], 0.0)
+    need("v", ip)
     cq = ts(T.cq[:, 0:1], T.ip[:, 0:1], 15, None, A.bitwise_and)
-    mpo = fill(T.poolw[:, :], 0)
-    need("v", cq)
-    sg = ts(T.sgf[:, :], T.sgi[:, :], 0.0, None, A.is_equal)
+    p15 = ts(T.p15[:, 0:1], T.ip[:, 0:1], 15.0, None, A.mult)
+    ch = ts(T.ch[:, 0:1], T.ip[:, 0:1], 1, 7, A.arith_shift_right, A.bitwise_and)
+    c1 = ts(T.c1[:, 0:1], T.ip[:, 0:1], 1, None, A.bitwise_and)
+    need("v", ic, p15)
+    sgi = ts(T.sgi[:, :], T.ic[:, :], 4, None, A.arith_shift_right)
     e8 = ts(T.e8[:, :], T.ic[:, :], T.p15[:, 0:1], 0.0, A.add, A.is_equal)
-    qf = V(v.tensor_copy(T.qf[:, 0:1], T.cq[:, 0:1]))
+    need("v", c1)
+    c8 = ts(T.c8[:, 0:1], T.c1[:, 0:1], 8.0, None, A.mult)
+    need("v", sgi)
+    sg = ts(T.sgf[:, :], T.sgi[:, :], 0.0, None, A.is_equal)
+    need("v", is1)
+    sa = ts(T.sa[:, :], T.is1[:, :], 2047, None, A.bitwise_and)
+    need("v", cq)
+    qf = copy(T.qf[:, 0:1], T.cq[:, 0:1])
+    need("v", ch, c8)
+    qs = tt(T.qs[:, 0:1], T.ch[:, 0:1], T.c8[:, 0:1], A.add)
+    need("v", sa)
+    sp = ts(T.sp[:, :], T.sa[:, :], -4095.5, None, A.add)
+    need("v", ij, qf)
+    mf = ts(T.maskf[:, :], T.ij[:, :], T.qf[:, 0:1], None, A.is_equal)
+    bf = ts(T.blkf[:, :], T.ij[:, :], 0.0, None, A.is_gt)
+    need("v", lmt)
+    mf_ = ts(T.mf[:, :], T.mt[:, :], 2.0 ** -11, 0.500244140625, A.mult, A.add)
+    mc = ts(T.mc[:, :], T.mt[:, :], 2047, None, A.bitwise_and)
+    need("v", lpl)
+    loi = ts(T.loi[:, :], T.pl[:, :], 7, None, A.bitwise_and)
+    lh = ts(T.lh[:, :], T.pl[:, :], 8, 8, A.arith_shift_right, A.bitwise_and)
+    need("v", mf_)
+    mff = copy(T.mff[:, :], T.mf[:, :])
+    need("v", mc, sp)
+    mn = tt(T.mn[:, :], T.mc[:, :], T.sp[:, :], A.subtract)
+    need("v", loi, lh)
+    lob = tt(T.lob[:, :], T.loi[:, :], T.lh[:, :], A.add)
+    need("v", mff)
+    mr = V(v.reciprocal(T.mr[:, :], T.mff[:, :]))
+    need("v", mn, mr)
+    mv = tt(T.mv[:, :], T.mn[:, :], T.mr[:, :], A.mult)
+    need("v", lzz)
+    zh = ts(T.zh[:, :], T.zz[:, :], 3, 255, A.arith_shift_right, A.bitwise_and)
+    need("v", mv)
+    mq = ts(T.mq[:, :], T.mv[:, :], -256.5, None, A.add)
     need("v", i4, i3o)
     n4i = ts(T.ind4i[:, :], T.i4[:, :], 31, 3, A.bitwise_and, A.arith_shift_right)
     i3i = ts(T.i32i[:, :], T.i3o[:, :], 231, None, A.bitwise_and)
-    fill(T.wina[:, 256:1152], 0)
-    need("v", i3i)
+    need("v", mq)
+    qb = copy(T.qb[:, :], T.mq[:, :])
+    need("v", n4i, i3i)
     n4 = ts(T.ind4[:, :], T.ind4i[:, :], 0.0, None, A.is_equal)
     i3 = ts(T.i32f[:, :], T.i32i[:, :], 128.0, None, A.is_equal)
-    need("v", lpl)
-    loi = ts(T.loi[:, :], T.pl[:, :], 7, None, A.bitwise_and)
-    need("v", lzz)
-    zh = ts(T.zh[:, :], T.zz[:, :], 3, None, A.arith_shift_right)
-    zq = ts(T.zq[:, :], T.zz[:, :], 7, None, A.arith_shift_right)
-    fill(T.wina[:, 1152:1600], 0)
-    need("v", zq)
-    lob = V(v.tensor_copy(T.lob[:, :], T.loi[:, :]))
-    zm = ts(T.zm[:, :], T.zq[:, :], 15.0, 8.0, A.min, A.mult)
-    mwa = fill(T.wina[:, 1600:2064], 0)
-    need("v", zm)
-    zc = tt(T.zc[:, :], T.zh[:, :], T.zm[:, :], A.add)
-    lz0 = fill(T.lz[:, :], 0.0)
-    ts(T.c7[:, 0:1], T.ip[:, 0:1], 7, None, A.bitwise_and)
-    c3 = ts(T.c3[:, 0:1], T.ip[:, 0:1], 3, 1, A.arith_shift_right, A.bitwise_and)
-    need("v", lz0, zc)
+    need("v", n4, zh, lz0)
     lz = None
     for b in range(8):
         h, bb = b // 4, b % 4
         c = 128 * h + 16 * b
-        lz = ts(T.lz[:, c:c + 16], T.zc[:, 16 * h:16 * h + 16], T.ind4[:, bb:bb + 1], None, A.mult)
-    need("v", ij)
-    mf = ts(T.maskf[:, :], T.ij[:, :], T.qf[:, 0:1], None, A.is_equal)
-    bf = ts(T.blkf[:, :], T.ij[:, :], 0.0, None, A.is_gt)
+        lz = ts(T.lz[:, c:c + 16], T.zh[:, 16 * h:16 * h + 16], T.ind4[:, bb:bb + 1], None, A.mult)
+    need("v", i1)
+    clist = copy(T.clist[:, :], T.i1[:, :])
     need("v", llt)
-    ltb = V(v.tensor_copy(T.ltb[:, :], T.lti[:, :]))
-    need("v", c3)
-    c16 = ts(T.c16[:, 0:1], T.c7[:, 0:1], 16.0, None, A.mult)
-    need("v", ia)
-    ts(T.lt[:, :], T.ia[:, :], 0.0, None, A.is_lt)
-    ts(T.ut[:, :], T.ia[:, :], 0.0, None, A.is_gt)
-    need("v", c16)
-    pcf = tt(T.pcf[:, 0:1], T.c16[:, 0:1], T.c3[:, 0:1], A.add)
-    ts(T.idn[:, :], T.ia[:, :], 0.0, None, A.is_equal)
-    ts(T.i8k[:, :], T.ia[:, :], 0.0, 8192.0, A.is_equal, A.mult)
-    fill(T.zer[:, :], 0.0)
-    fill(T.n64[:, :], -64.0)
-    con = fill(T.bw[:, 0:1], 0.0)
-    need("v", pcf, i2)
-    permo = ts(T.permo[:, :], T.i2[:, :], T.pcf[:, 0:1], None, A.add)
+    ltb = copy(T.ltb[:, :], T.lti[:, :])
+    i128 = fill(T.i128[:, :], 1.0 / 128)
 
-    need("t", lz, i3)
-    te.matmul(T.psz[:, 0:32], T.lz[:, 0:128], T.i32f[:, :], True, False)
-    pz = P(te.matmul(T.psz[:, 0:32], T.lz[:, 128:256], T.i32f[:, :], False, True))
     for s in range(4):
         dlo = dma("y", T.lor[:, 128 * s:128 * s + 128], T.lob[32 * s:32 * s + 32, :], "dlo", lob)
     need("t", dlo, e8)
     plo = P(te.matmul(T.ps4[:, :], T.e8[0:8, :], T.lor[:, :], True, True))
-    need("v", pz)
-    offm = ts(T.offm[:, :], T.psz[:, 0:32], 8.0, None, A.add)
-    need("v", plo)
-    selm = ts(T.selm[:, :], T.ps4[:, :], T.qf[:, 0:1], None, A.is_equal)
+    need("t", lz, i3)
+    te.matmul(T.psz[:, 0:32], T.lz[:, 0:128], T.i32f[:, :], True, False)
+    pz = P(te.matmul(T.psz[:, 0:32], T.lz[:, 128:256], T.i32f[:, :], False, True))
+    need("v", plo, qs)
+    selm = ts(T.selm[:, :], T.ps4[:, :], T.qs[:, 0:1], None, A.is_equal)
+
+    dth = dma("y", T.snd2[:, :, :], T.qb[:, :], "dth", qb)
+    dow2 = dma("y", T.land2[me, :, :], T.qb[16 * me:16 * me + 16, :], "dow2")
+    need("g", dth)
+    a2 = send(T.snd2, T.land2, "a2")
+    choose(T.idn[:, :], T.c255[:, :], -1, A.is_equal, 1, n255)
+    nid = choose(T.nid[:, :], T.n255[:, :], -1, A.is_equal, 1)
 
     need("s", ones, sg)
-    se = None
     for b in range(8):
-        se = act(T.selw[:, 128 * b:128 * b + 128], T.ones[:, :], 0.0, T.sgf[:, 16 * b:16 * b + 1])
+        act(T.selw[:, 128 * b:128 * b + 128], T.ones[:, :], 0.0, T.sgf[:, 16 * b:16 * b + 1])
+    se = act(T.sgb[:, :], T.sgf[:, :])
+    need("s", se)
+    act(T.lw[:, 0:1024], T.selw[:, :])
+
+    need("s", a0, own0)
+    dst = dma("y", T.c0[:, :], T.land0[:, 0:16, :], "dst", a0, own0)
+    for b in range(4):
+        dpb = dma("s", T.poolw[16 * b:16 * b + 16, :], T.land0[:, 16:80, :], "dpb")
+        dpa = dma("y", T.poolw[16 * b + 64:16 * b + 80, :], T.land0[:, 16:80, :], "dpa")
+    dwa = dma("y", T.wq[:, :], T.land1[:, :, :], "dwa", a1, own1)
+    for q in range(16):
+        dw = dma("y", T.win[q:128:16, :], T.land1[:, :, :], "dw")
     need("s", mf, bf)
-    act(T.maskb[:, :], T.maskf[:, :])
-    mb = act(T.blkb[:, :], T.blkf[:, :])
+    mb = act(T.maskb[:, :], T.maskf[:, :])
+    bb = act(T.blkb[:, :], T.blkf[:, :])
     dlt = dma("s", T.snd3[:, :, :], T.ltb[:, :], "dlt", ltb)
     dow3 = dma("s", T.land3[me, :, :], T.ltb[16 * me:16 * me + 16, :], "dow3")
     need("g", dlt)
     a3 = send(T.snd3, T.land3, "a3")
-
-    need("y", a1, own, mpo, mwa)
-    need("s", a1, own, mpo)
-    dst = dma("y", T.c0[:, :], T.land1[:, 0:16, 0:8], "dst")
-    dwa = dma("y", T.wina[0:128:16, :], T.land1[:, 26:112, :], "dwa")
-    for b in range(4):
-        dpb = dma("s", T.poolw[16 * b:16 * b + 8, :], T.land1[:, 0:27, :], "dpb")
-        dpa = dma("y", T.poolw[16 * b + 64:16 * b + 72, :], T.land1[:, 0:27, :], "dpa")
-    for q in range(16):
-        dw = dma("y", T.win[q:128:16, :], T.land1[:, 26:112, :], "dw")
-    need("s", se)
-    act(T.lw[:, 0:1024], T.selw[:, :])
-    act(T.lw[:, 2048:2064], T.selw[:, 0:16])
     lwf = act(T.lw[:, 1024:2048], T.selw[:, :])
-    dlw = dma("y", T.lw[0:128:16, 16:2064], T.land3[:, :, :], "dlw", a3, dow3, lwf)
 
     need("v", dst)
+    kt = ts(T.k[:, :], T.c0[:, :], 7, 15, A.arith_shift_right, A.bitwise_and)
+    lo = ts(T.lo[:, :], T.c0[:, :], 127, None, A.bitwise_and)
     sl = ts(T.sl[:, :], T.c0[:, :], 2047, None, A.bitwise_and)
+    need("v", kt, mf, clist)
+    km = tt(T.km[:, :], T.k[:, :].indirect(T.clist[:, :]), T.maskf[:, :], A.mult)
+    need("t", km, se)
+    pk = P(te.matmul(T.psb[:, 0:128], T.sgb[:, :], T.km[:, :], True, True))
+    need("v", lo)
+    off0 = copy(T.off0[:, :], T.lo[:, :])
     h2 = ts(T.h2[:, :], T.c0[:, :], 2.0 ** -11, 2047.500244140625, A.mult, A.add)
+    need("v", pz)
+    offm = copy(T.offm[:, :], T.psz[:, 0:32])
 
-    gby, segc, offs = {}, {}, {}
+    gby, segc, offs, ends = {}, {}, {}, {}
 
     def gather(s0, s1):
         r = tt(T.gby[:, 128 * s0:128 * s1], T.poolw[:, :].indirect(T.offm[:, 8 * s0:8 * s1]),
@@ -247,81 +286,136 @@ def rank_program(g, core, T, topo):
         need("s", act(lg, T.lw[:, :].indirect(T.off[:, 8 * s:8 * s + 8])))
         return act(T.outs[:, 128 * s:128 * s + 128], lg.indirect(T.permo[:, :]))
 
-    prev = offm
+    prev, py = None, None
     for s in range(4):
-        c = 8 * s
+        c, x = 8 * s, 144 * (s - 1)
+        E = T.sc[:, 15:128:16]
         need("v", sl)
-        offs[s] = ts(T.off[:, c:c + 8], T.sl[:, :], 16.0, None, A.add)
-        need("v", offs[s])
+        offs[s] = copy(T.off[:, c:c + 8], T.sl[:, :])
+        slm = ts(T.slm[:, :], T.sl[:, :], -2048.0, None, A.add)
+        if s > 0:
+            need("t", prev, ones)
+            for j in range(s):
+                te.matmul(T.psb[:, 0:1], T.ones[:, :], ends[j], j == 0, False)
         if s == 0:
-            need("v", dwa)
-            t = V(v.tensor_copy(T.g0[:, :], T.wina[:, :].indirect(T.off[:, c:c + 8])))
+            need("v", pk)
+            selx = ts(T.selx[:, :], T.psb[:, 0:128], T.qf[:, 0:1], None, A.is_equal)
+            need("v", off0, selx, dwa)
+            t = tt(T.g0[:, :], T.wq[:, :].indirect(T.off0[:, :]), T.selx[:, :], A.mult)
             need("t", t, sg)
             t = P(te.matmul(T.psr[:, 0:128], T.sgf[:, :], T.g0[:, :], True, True))
             need("v", dpa, dpb, offm, selm)
             gather(0, 1)
-            gather(1, 3)
             segment(0)
             segment(1)
+            gather(1, 3)
             need("v", t, mf)
-            gm = tt(T.gm[:, :], T.psr[:, 0:128], T.maskf[:, :], A.mult)
+            py = gm = tt(T.gm[:, :], T.psr[:, 0:128], T.maskf[:, :], A.mult)
+            zer = fill(T.zer[:, :], 0.0)
+            need("v", gm, bf)
+            e = scan(T.sc[:, :], T.blkf[:, :], T.gm[:, :], A.mult, A.add)
+            bm = ts(T.bmask[:, :], T.maskf[:, :], -6400.0, 4096.0, A.mult, A.add)
+            zp = fill(T.ppx[:, 15:432:144], 0.0)
+            need("v", e)
+            f3 = ts(T.f3[:, :], E, 2.0 ** -11, 0.500244140625, A.mult, A.add)
+            need("v", slm)
+            u = tt(T.u[:, :], T.slm[:, :], E, A.subtract)
+            c7 = ts(T.c7[:, 0:1], T.ip[:, 0:1], 7, None, A.bitwise_and)
+            need("v", f3, h2)
+            pr = tt(T.pr[:, :], T.f3[:, :], T.h2[:, :], A.mult)
+            need("v", u)
+            u4 = ts(T.u4[:, :], T.u[:, :], -1.0, 4096.0, A.mult, A.add)
+            con = fill(T.bw[:, 0:1], 0.0)
+            need("v", pr, u4)
+            w = tt(T.w[:, :], T.pr[:, :], T.u4[:, :], A.is_lt)
+            xq = tt(T.xq[:, :], T.pr[:, :], T.u[:, :], A.add)
+            need("v", w, zer)
+            ppc, ends[s] = T.pp[:, :], T.pp[:, 7:8]
+            pp = scan(ppc, T.w[:, :], T.zer[:, 0:8], A.add, A.max)
+            g256 = ts(T.g256[:, :], T.w[:, :], 255.0, 1.0, A.mult, A.add)
+            need("v", clist, mb)
+            wm = tt(T.wm[:, :], T.w[:, :].indirect(T.clist[:, :]), T.maskb[:, :], A.mult)
         else:
-            need("v", dw)
+            need("v", offs[s], hx, dw)
             gm = tt(T.gm[:, :], T.win[:, :].indirect(T.off[:, c:c + 8]), T.maskf[:, :], A.mult)
-            h2 = ts(T.h2[:, :], T.y[:, :], 2.0 ** -11, 2046.500244140625, A.mult, A.add)
-        need("v", gm, bf)
-        e = V(v.tensor_tensor_scan(T.sc[:, :], T.blkf[:, :], T.gm[:, :], 0.0, A.mult, A.add))
-        need("v", e)
-        E = T.sc[:, 15:128:16]
-        f3 = ts(T.f3[:, :], E, 2.0 ** -11, 0.500244140625, A.mult, A.add)
-        u = tt(T.u[:, :], T.sl[:, :], E, A.subtract)
-        need("v", f3, h2)
-        pr = tt(T.pr[:, :], T.f3[:, :], T.h2[:, :], A.mult)
-        need("v", u)
-        u4 = ts(T.u4[:, :], T.u[:, :], -1.0, 6144.0, A.mult, A.add)
-        need("t", prev, con)
-        te.matmul(T.psz[:, 0:8], T.ones[:, :], T.n64[:, :], True, False)
+            need("v", dtw)
+            wm = tt(T.wm[:, :], T.thw[:, :].indirect(T.off[:, c:c + 8]), T.hxm[:, :], A.is_ge)
+            need("v", gm)
+            e = scan(T.sc[:, :], T.blkf[:, :], T.gm[:, :], A.mult, A.add)
+            need("v", wm)
+            pp = scan(T.ppx[:, x + 16:x + 144], T.wm[:, :], T.zer[:, :], A.add, A.max)
+            ppc, ends[s] = T.ppx[:, x + 31:x + 144:16], T.ppx[:, x + 143:x + 144]
+            need("v", e)
+            f3 = ts(T.f3[:, :], E, 2.0 ** -11, 0.500244140625, A.mult, A.add)
+            need("v", slm)
+            u = tt(T.u[:, :], T.slm[:, :], E, A.subtract)
+            need("v", f3, h2)
+            pr = tt(T.pr[:, :], T.f3[:, :], T.h2[:, :], A.mult)
+        need("t", pp, lt)
+        base = P(te.matmul(T.psb[:, 0:1], T.lt[:, :], ends[s], s == 0, True))
+        if s == 0:
+            segment(2)
+            segment(3)
+            need("v", xq, g256)
+            y = tt(T.y[:, :], T.xq[:, :], T.g256[:, :], A.mult)
+        else:
+            need("t", i128, nid, zp, py)
+            te.matmul(T.psr[:, 0:8], T.idn[:, :], ppc, True, False)
+            te.matmul(T.psr[:, 0:8], T.nid[:, :], T.ppx[:, x + 15:x + 128:16], False, False)
+            pg = P(te.matmul(T.psr[:, 0:8], T.ones[:, :], T.i128[:, :], False, True))
+        need("v", base, con)
+        prev = ts(T.off2[:, c:c + 8], ppc, T.psb[:, 0:1], None, A.add)
         if s > 0:
-            te.matmul(T.psb[:, 0:1], T.ut[:, :], T.pp[:, c - 1:c], True, False)
-        need("v", pr, u4)
-        w = tt(T.w[:, :], T.pr[:, :], T.u4[:, :], A.is_lt)
-        xq = tt(T.xq[:, :], T.pr[:, :], T.u[:, :], A.add)
-        need("v", w)
-        ini = 0.0 if s == 0 else T.pp[:, c - 1:c]
-        pp = V(v.tensor_tensor_scan(T.pp[:, c:c + 8], T.w[:, :], T.zer[:, :], ini, A.add, A.max))
-        need("t", w)
-        te.matmul(T.psz[:, 0:8], T.i8k[:, :], T.w[:, :], False, False)
-        need("t", pp)
-        te.matmul(T.psb[:, 0:1], T.lt[:, :], T.pp[:, c + 7:c + 8], s == 0, True)
-        base = P(te.matmul(T.psz[:, 0:8], T.idn[:, :], T.pp[:, c:c + 8], False, True))
-        need("v", xq)
-        n = ts(T.n[:, :], T.xq[:, :], -2048.0, 255.0, A.add, A.mult)
+            need("v", pr, u)
+            xq = tt(T.xq[:, :], T.pr[:, :], T.u[:, :], A.add)
+        else:
+            need("v", y)
+            h2 = ts(T.h2[:, :], T.y[:, :], 2.0 ** -11, 2047.500244140625, A.mult, A.add)
+            y2 = ts(T.ylo[:, :], T.y[:, :], 2047, None, A.bitwise_and)
+        need("v", prev, wm, segc[2 * s + 1])
+        t = tt(T.gb[:, :], T.bw[:, 0:1025 + 1024 * s].indirect(T.off2[:, c:c + 8]), T.wm[:, :], A.mult)
+        if s > 0:
+            need("v", xq, pg)
+            py = y = tt(T.y[:, :], T.xq[:, :], T.psr[:, 0:8], A.mult)
+        if s == 1:
+            need("v", i2, pcf)
+            permo = ts(T.permo[:, :], T.i2[:, :], T.pcf[:, 0:1], None, A.add)
         if s == 0:
             gather(3, 4)
-        need("v", n)
-        m = tt(T.m[:, :], T.n[:, :], T.w[:, :], A.mult)
-        need("v", base)
-        prev = ts(T.off2[:, c:c + 8], T.psz[:, 0:8], T.psb[:, 0:1], 0.0, A.add, A.max)
-        need("v", m)
-        y = tt(T.y[:, :], T.m[:, :], T.xq[:, :], A.add)
-        need("v", prev, mb, con, segc[2 * s + 1])
-        t = tt(T.gb[:, :], T.bw[:, 0:1025 + 1024 * s].indirect(T.off2[:, c:c + 8]), T.maskb[:, :], A.mult)
-        need("v", y)
-        if s < 3:
-            y2 = ts(T.ylo[:, :], T.y[:, :], 2047, None, A.bitwise_and)
-        else:
-            y2 = ts(T.yt[:, :], T.y[:, :], -2048.0, None, A.add)
-        need("v", t)
-        t = V(v.tensor_tensor_scan(T.sb[:, :], T.blkb[:, :], T.gb[:, :], 0.0, A.mult, A.add))
-        need("v", t, y2)
-        if s < 3:
-            sl = tt(T.sl[:, :], T.ylo[:, :], T.sb[:, 15:128:16], A.add)
-            segment(2 * s + 2)
-            segment(2 * s + 3)
-        else:
-            xl = tt(T.xl[:, :], T.yt[:, :], T.sb[:, 15:128:16], A.add)
+            c3 = ts(T.c3[:, 0:1], T.ip[:, 0:1], 3, 1, A.arith_shift_right, A.bitwise_and)
+        need("v", t, bb)
+        t = scan(T.sb[:, :], T.blkb[:, :], T.gb[:, :], A.mult, A.add)
+        if s == 3:
+            need("v", t, y)
+            xl = tt(T.xl[:, :], T.y[:, :], T.sb[:, 15:128:16], A.add)
+            break
         if s > 0:
-            letters(s - 1)
+            need("v", y)
+            y2 = ts(T.ylo[:, :], T.y[:, :], 2047, None, A.bitwise_and)
+            h2 = ts(T.h2[:, :], T.y[:, :], 2.0 ** -11, 2047.500244140625, A.mult, A.add)
+        else:
+            need("v", c7)
+            c16 = ts(T.c16[:, 0:1], T.c7[:, 0:1], 16.0, None, A.mult)
+        need("v", t, y2)
+        sl = tt(T.sl[:, :], T.ylo[:, :], T.sb[:, 15:128:16], A.add)
+        if s == 0:
+            need("v", c16, c3)
+            pcf = tt(T.pcf[:, 0:1], T.c16[:, 0:1], T.c3[:, 0:1], A.add)
+        need("v", h2, bm)
+        hx = tt(T.hxm[:, :], T.h2[:, :].indirect(T.clist[:, :]), T.bmask[:, :], A.add)
+        if s == 0:
+            for q in range(16):
+                dtw = dma("y", T.thw[q:128:16, :], T.land2[:, :, :], "dtw", a2, dow2)
+            dlw = dma("y", T.lw[0:128:16, :], T.land3[:, :, :], "dlw", a3, dow3, lwf)
+            segment(4)
+            segment(5)
+        elif s == 1:
+            segment(6)
+            segment(7)
+            letters(0)
+        else:
+            letters(1)
+            letters(2)
     outs = letters(3)
 
     dsy = dma("s", T.snd4[:, :, :], T.outs[0:128:16, :], "dsy", outs)

from concourse.bass import DstId, RemoteDMATransfer
from concourse.mybir import AluOpType as A, ActivationFunctionType as F

I32, U16, F32, B16 = "int32", "uint16", "float32", "bfloat16"
SCRATCH = {}
for _i, _w, _t in ((0, 8, I32), (1, 16, I32), (2, 16, B16), (3, 16, B16), (4, 4, F32), (5, 1, F32)):
    SCRATCH["snd%d" % _i] = SCRATCH["land%d" % _i] = ("dram", [8, 128, _w], _t)
for _t, _l in (
        (I32, "ic 128 ij 128 is1 128 ip 8 i2 8 i1 8 i4 4 i3o 32 cq 8 c7 8 c3 8 ch 8 c1 8 c8 8 sgi 128 i32i 32"
              " ind4i 4 pl 32 zz 32 zh 32 loi 32 lh 32 poolw 256 wq 128 win 2048 lti 128 c0 8 k 8 lo 8 f3 8 h2 8"
              " y 8 ylo 8 sl 8 mt 128 mf 128 mc 128 mq 128 sa 128"),
        (U16, "permo 8 clist 8 offm 32 off 32 off0 8 off2 32"),
        (F32, "qf 8 qs 8 p15 8 c16 8 pcf 8 maskf 128 blkf 128 bmask 128 hxm 128 sgf 128 i32f 32 ind4 4 lz 256 selx 128 g0 128"
              " gm 128 sc 128 slm 8 u 8 u4 8 pr 8 xq 8 g256 8 xl 8 lg 512 outs 512 sp 128 mff 128 mn 128 mr 128 mv 128"),
        (B16, "blkb 128 lt 128 e8 128 ones 128 c255 128 n255 128 idn 128 nid 128 i128 8 selw 1024 sgb 128 km 128 zer 128"
              " lob 32 selm 512 gby 512 bw 4112 ltb 128 lw 2048 thw 2048 qb 128 maskb 128 w 8 wm 128 pp 8 ppx 432 sb 128"
              " gb 128")):
    _l = _l.split()
    for _i in range(0, len(_l), 2):
        SCRATCH[_l[_i]] = ("sbuf", [128, int(_l[_i + 1])], _t)
SCRATCH["lor"] = ("sbuf", [8, 512], B16)
for _i in ("ps0", "ps1", "ps2", "ps3", "ps4", "psr", "psz", "psb"):
    SCRATCH[_i] = ("psum", [128, 512], F32)
SEMAPHORES = ["gi", "v", "t", "s", "ls", "a0", "a1", "a2", "a3", "a4", "a5",
              "l0", "l1", "own0", "own1", "lmt", "lpl", "lzz", "llt", "dlo", "dth", "dlt", "dow2", "dow3", "dst", "dpa",
              "dpb", "dwa", "dw", "dtw", "dlw", "dsy", "dow4", "dla", "dow5", "fsy", "fla"]


def rank_program(g, core, T, topo):
    me = T.rank_of(core)
    if me is None:
        return
    Q = {"g": g, "v": g.vector, "s": g.scalar, "y": g.sync, "t": g.tensor}
    cnt, seen, waited = {}, {}, {}

    def did(ins, sem, n=1):
        ins.then_inc(T.sem[sem], n)
        cnt[sem] = cnt.get(sem, 0) + n
        return (sem, cnt[sem])

    def need(q, *toks):
        for sem, val in toks:
            if seen.get((q, sem), 0) < val:
                Q[q].wait_ge(T.sem[sem], val)
                seen[(q, sem)] = val
                waited[sem] = max(waited.get(sem, 0), val)

    v, ac, te = g.vector, g.scalar, g.tensor

    def dma(q, out, in_, sem, *toks):
        need(q, *toks)
        return did(Q[q].dma_start(out, in_), sem, 16)

    def V(ins):
        return did(ins, "v")

    def S(ins):
        return did(ins, "s")

    def P(ins):
        return did(ins, "t")

    def ts(out, in_, s1, s2, o1, *o2):
        return V(v.tensor_scalar(out, in_, s1, s2, o1, *o2))

    def tt(out, a, b, op):
        return V(v.tensor_tensor(out, a, b, op))

    def scan(out, a, b, o1, o2):
        return V(v.tensor_tensor_scan(out, a, b, 0.0, o1, o2))

    def copy(out, in_):
        return V(v.tensor_copy(out, in_))

    def fill(ap, x):
        return V(v.memset(ap, x))

    def act(out, in_, *sc):
        return S(ac.activation(out, in_, F.Copy, *sc))

    others = [d for d in T.cores if d != core]
    near = topo.cores_of(core)
    eng, k, kk = {}, 0, 0
    for d in others:
        es = topo.engines(core, d)
        if d in near:
            kk += 1
            eng[d] = es[-kk]
        else:
            eng[d] = (es[0::2] + es[1::2])[k]
            k += 1

    def send(src, dst, arr):
        tr = []
        for d in others:
            rid, pnc = topo.addr(d, core)
            tr.append(RemoteDMATransfer(dst_ids=[DstId(rid=rid, pnc=pnc)], dma_engine_mask=1 << eng[d],
                                        remote_sem=T.sem[arr], src=src[T.rank_of(d)], dst=dst[me]))
        g.remote_dma_fused(tr, local_sem=T.sem.ls)
        cnt["ls"] = cnt.get("ls", 0) + len(tr)
        cnt[arr] = len(others)
        return (arr, len(others))

    dma("s", T.snd0[:, 0:16, :], T.states[:, :], "l0")
    dma("y", T.snd0[:, 16:80, :], T.stock[:, :], "l0")
    l0 = dma("s", T.snd0[:, 80:128, :], T.models[:, 0:384], "l0")
    l1 = dma("y", T.snd1[:, :, :], T.models[:, :], "l1")
    lmt = dma("y", T.mt[:, :], T.models[:, :], "lmt")
    lpl = dma("y", T.pl[:, :], T.places[me, :], "lpl")
    for s in range(4):
        for h in range(2):
            t = 1024 * s + 512 * h
            lzz = dma("s", T.zz[32 * s:32 * s + 32, 16 * h:16 * h + 16], T.places[me, t:t + 512], "lzz")
    llt = dma("y", T.lti[:, :], T.letters[:, :], "llt")
    dma("y", T.land0[me, 0:16, :], T.states[me, :], "own0")
    own0 = dma("y", T.land0[me, 16:80, :], T.stock[me, :], "own0")
    own1 = dma("y", T.land1[me, :, :], T.models[me, :], "own1")

    def pattern(out, pat, base, mul):
        return did(g.iota(out, pat, base, mul), "gi")

    def choose(out, in_, step, op, mul, *toks):
        need("g", *toks)
        return did(g.affine_select(out, in_, [[step, 128]], op, 0.0, 0, mul), "gi")

    ip = pattern(T.ip[:, 0:1], [[0, 1]], 0, 1)
    ic = pattern(T.ic[:, :], [[-16, 8], [0, 16]], 0, 1)
    is1 = pattern(T.is1[:, :], [[1, 128]], 0, 128)
    ij = pattern(T.ij[:, :], [[0, 8], [1, 16]], 0, 0)
    need("g", l0)
    a0 = send(T.snd0, T.land0, "a0")
    need("g", l1)
    a1 = send(T.snd1, T.land1, "a1")
    i4 = pattern(T.i4[:, :], [[-8, 4]], 0, 1)
    i3o = pattern(T.i3o[:, :], [[-32, 4], [-1, 8]], 128, 1)
    i1 = pattern(T.i1[:, :], [[1, 8]], 0, 0)
    i2 = pattern(T.i2[:, :], [[2, 8]], 0, 0)

    ones = fill(T.ones[:, :], 1.0)
    fill(T.c255[:, :], 255.0)
    n255 = fill(T.n255[:, :], -255.0)
    lt = choose(T.lt[:, :], T.ones[:, :], 1, A.is_gt, -1, ones)
    lz0 = fill(T.lz[:, :], 0.0)
    need("v", ip)
    cq = ts(T.cq[:, 0:1], T.ip[:, 0:1], 15, None, A.bitwise_and)
    p15 = ts(T.p15[:, 0:1], T.ip[:, 0:1], 15.0, None, A.mult)
    ch = ts(T.ch[:, 0:1], T.ip[:, 0:1], 1, 7, A.arith_shift_right, A.bitwise_and)
    c1 = ts(T.c1[:, 0:1], T.ip[:, 0:1], 1, None, A.bitwise_and)
    need("v", ic, p15)
    sgi = ts(T.sgi[:, :], T.ic[:, :], 4, None, A.arith_shift_right)
    e8 = ts(T.e8[:, :], T.ic[:, :], T.p15[:, 0:1], 0.0, A.add, A.is_equal)
    need("v", c1)
    c8 = ts(T.c8[:, 0:1], T.c1[:, 0:1], 8.0, None, A.mult)
    need("v", sgi)
    sg = ts(T.sgf[:, :], T.sgi[:, :], 0.0, None, A.is_equal)
    need("v", is1)
    sa = ts(T.sa[:, :], T.is1[:, :], 2047, None, A.bitwise_and)
    need("v", cq)
    qf = copy(T.qf[:, 0:1], T.cq[:, 0:1])
    need("v", ch, c8)
    qs = tt(T.qs[:, 0:1], T.ch[:, 0:1], T.c8[:, 0:1], A.add)
    need("v", sa)
    sp = ts(T.sp[:, :], T.sa[:, :], -4095.5, None, A.add)
    need("v", ij, qf)
    mf = ts(T.maskf[:, :], T.ij[:, :], T.qf[:, 0:1], None, A.is_equal)
    bf = ts(T.blkf[:, :], T.ij[:, :], 0.0, None, A.is_gt)
    need("v", lmt)
    mf_ = ts(T.mf[:, :], T.mt[:, :], 2.0 ** -11, 0.500244140625, A.mult, A.add)
    mc = ts(T.mc[:, :], T.mt[:, :], 2047, None, A.bitwise_and)
    need("v", lpl)
    loi = ts(T.loi[:, :], T.pl[:, :], 7, None, A.bitwise_and)
    lh = ts(T.lh[:, :], T.pl[:, :], 8, 8, A.arith_shift_right, A.bitwise_and)
    need("v", mf_)
    mff = copy(T.mff[:, :], T.mf[:, :])
    need("v", mc, sp)
    mn = tt(T.mn[:, :], T.mc[:, :], T.sp[:, :], A.subtract)
    need("v", loi, lh)
    lob = tt(T.lob[:, :], T.loi[:, :], T.lh[:, :], A.add)
    need("v", mff)
    mr = V(v.reciprocal(T.mr[:, :], T.mff[:, :]))
    need("v", mn, mr)
    mv = tt(T.mv[:, :], T.mn[:, :], T.mr[:, :], A.mult)
    need("v", lzz)
    zh = ts(T.zh[:, :], T.zz[:, :], 3, 255, A.arith_shift_right, A.bitwise_and)
    need("v", mv)
    mq = ts(T.mq[:, :], T.mv[:, :], -256.5, None, A.add)
    need("v", i4, i3o)
    n4i = ts(T.ind4i[:, :], T.i4[:, :], 31, 3, A.bitwise_and, A.arith_shift_right)
    i3i = ts(T.i32i[:, :], T.i3o[:, :], 231, None, A.bitwise_and)
    need("v", mq)
    qb = copy(T.qb[:, :], T.mq[:, :])
    need("v", n4i, i3i)
    n4 = ts(T.ind4[:, :], T.ind4i[:, :], 0.0, None, A.is_equal)
    i3 = ts(T.i32f[:, :], T.i32i[:, :], 128.0, None, A.is_equal)
    need("v", n4, zh, lz0)
    lz = None
    for b in range(8):
        h, bb = b // 4, b % 4
        c = 128 * h + 16 * b
        lz = ts(T.lz[:, c:c + 16], T.zh[:, 16 * h:16 * h + 16], T.ind4[:, bb:bb + 1], None, A.mult)
    need("v", i1)
    clist = copy(T.clist[:, :], T.i1[:, :])
    need("v", llt)
    ltb = copy(T.ltb[:, :], T.lti[:, :])
    i128 = fill(T.i128[:, :], 1.0 / 128)

    for s in range(4):
        dlo = dma("y", T.lor[:, 128 * s:128 * s + 128], T.lob[32 * s:32 * s + 32, :], "dlo", lob)
    need("t", dlo, e8)
    plo = P(te.matmul(T.ps4[:, :], T.e8[0:8, :], T.lor[:, :], True, True))
    need("t", lz, i3)
    te.matmul(T.psz[:, 0:32], T.lz[:, 0:128], T.i32f[:, :], True, False)
    pz = P(te.matmul(T.psz[:, 0:32], T.lz[:, 128:256], T.i32f[:, :], False, True))
    need("v", plo, qs)
    selm = ts(T.selm[:, :], T.ps4[:, :], T.qs[:, 0:1], None, A.is_equal)

    dth = dma("y", T.snd2[:, :, :], T.qb[:, :], "dth", qb)
    dow2 = dma("y", T.land2[me, :, :], T.qb[16 * me:16 * me + 16, :], "dow2")
    need("g", dth)
    a2 = send(T.snd2, T.land2, "a2")
    choose(T.idn[:, :], T.c255[:, :], -1, A.is_equal, 1, n255)
    nid = choose(T.nid[:, :], T.n255[:, :], -1, A.is_equal, 1)

    need("s", ones, sg)
    for b in range(8):
        act(T.selw[:, 128 * b:128 * b + 128], T.ones[:, :], 0.0, T.sgf[:, 16 * b:16 * b + 1])
    se = act(T.sgb[:, :], T.sgf[:, :])
    need("s", se)
    act(T.lw[:, 0:1024], T.selw[:, :])

    need("s", a0, own0)
    dst = dma("y", T.c0[:, :], T.land0[:, 0:16, :], "dst", a0, own0)
    for b in range(4):
        dpb = dma("s", T.poolw[16 * b:16 * b + 16, :], T.land0[:, 16:80, :], "dpb")
        dpa = dma("y", T.poolw[16 * b + 64:16 * b + 80, :], T.land0[:, 16:80, :], "dpa")
    dwa = dma("y", T.wq[:, :], T.land1[:, :, :], "dwa", a1, own1)
    for q in range(16):
        dw = dma("y", T.win[q:128:16, :], T.land1[:, :, :], "dw")
    need("s", mf, bf)
    mb = act(T.maskb[:, :], T.maskf[:, :])
    bb = act(T.blkb[:, :], T.blkf[:, :])
    dlt = dma("s", T.snd3[:, :, :], T.ltb[:, :], "dlt", ltb)
    dow3 = dma("s", T.land3[me, :, :], T.ltb[16 * me:16 * me + 16, :], "dow3")
    need("g", dlt)
    a3 = send(T.snd3, T.land3, "a3")
    lwf = act(T.lw[:, 1024:2048], T.selw[:, :])

    need("v", dst)
    kt = ts(T.k[:, :], T.c0[:, :], 7, 15, A.arith_shift_right, A.bitwise_and)
    lo = ts(T.lo[:, :], T.c0[:, :], 127, None, A.bitwise_and)
    sl = ts(T.sl[:, :], T.c0[:, :], 2047, None, A.bitwise_and)
    need("v", kt, mf, clist)
    km = tt(T.km[:, :], T.k[:, :].indirect(T.clist[:, :]), T.maskf[:, :], A.mult)
    need("t", km, se)
    pk = P(te.matmul(T.psb[:, 0:128], T.sgb[:, :], T.km[:, :], True, True))
    need("v", lo)
    off0 = copy(T.off0[:, :], T.lo[:, :])
    h2 = ts(T.h2[:, :], T.c0[:, :], 2.0 ** -11, 2047.500244140625, A.mult, A.add)
    need("v", pz)
    offm = copy(T.offm[:, :], T.psz[:, 0:32])

    gby, segc, offs, ends = {}, {}, {}, {}

    def gather(s0, s1):
        r = tt(T.gby[:, 128 * s0:128 * s1], T.poolw[:, :].indirect(T.offm[:, 8 * s0:8 * s1]),
               T.selm[:, 128 * s0:128 * s1], A.mult)
        for s in range(s0, s1):
            gby[s] = r

    def segment(i):
        ps = T["ps%d" % (i % 5)]
        s, p = i // 2, None
        need("t", gby[s], se)
        if i >= 5:
            need("t", segc[i - 5])
        for k in range(4):
            b = 4 * (i % 2) + k
            p = P(te.matmul(ps[:, 128 * k:128 * k + 128], T.selw[:, 128 * b:128 * b + 128],
                            T.gby[:, 128 * s:128 * s + 128], True, True))
        need("s", p)
        segc[i] = act(T.bw[:, 1 + 512 * i:513 + 512 * i], ps[:, :])

    def letters(s):
        need("s", offs[s], dlw, permo)
        lg = T.lg[:, 128 * s:128 * s + 128]
        need("s", act(lg, T.lw[:, :].indirect(T.off[:, 8 * s:8 * s + 8])))
        return act(T.outs[:, 128 * s:128 * s + 128], lg.indirect(T.permo[:, :]))

    prev, py = None, None
    for s in range(4):
        c, x = 8 * s, 144 * (s - 1)
        E = T.sc[:, 15:128:16]
        need("v", sl)
        offs[s] = copy(T.off[:, c:c + 8], T.sl[:, :])
        slm = ts(T.slm[:, :], T.sl[:, :], -2048.0, None, A.add)
        if s > 0:
            need("t", prev, ones)
            for j in range(s):
                te.matmul(T.psb[:, 0:1], T.ones[:, :], ends[j], j == 0, False)
        if s == 0:
            need("v", pk)
            selx = ts(T.selx[:, :], T.psb[:, 0:128], T.qf[:, 0:1], None, A.is_equal)
            need("v", off0, selx, dwa)
            t = tt(T.g0[:, :], T.wq[:, :].indirect(T.off0[:, :]), T.selx[:, :], A.mult)
            need("t", t, sg)
            t = P(te.matmul(T.psr[:, 0:128], T.sgf[:, :], T.g0[:, :], True, True))
            need("v", dpa, dpb, offm, selm)
            gather(0, 1)
            segment(0)
            segment(1)
            gather(1, 3)
            need("v", t, mf)
            py = gm = tt(T.gm[:, :], T.psr[:, 0:128], T.maskf[:, :], A.mult)
            zer = fill(T.zer[:, :], 0.0)
            need("v", gm, bf)
            e = scan(T.sc[:, :], T.blkf[:, :], T.gm[:, :], A.mult, A.add)
            bm = ts(T.bmask[:, :], T.maskf[:, :], -6400.0, 4096.0, A.mult, A.add)
            zp = fill(T.ppx[:, 15:432:144], 0.0)
            need("v", e)
            f3 = ts(T.f3[:, :], E, 2.0 ** -11, 0.500244140625, A.mult, A.add)
            need("v", slm)
            u = tt(T.u[:, :], T.slm[:, :], E, A.subtract)
            c7 = ts(T.c7[:, 0:1], T.ip[:, 0:1], 7, None, A.bitwise_and)
            need("v", f3, h2)
            pr = tt(T.pr[:, :], T.f3[:, :], T.h2[:, :], A.mult)
            need("v", u)
            u4 = ts(T.u4[:, :], T.u[:, :], -1.0, 4096.0, A.mult, A.add)
            con = fill(T.bw[:, 0:1], 0.0)
            need("v", pr, u4)
            w = tt(T.w[:, :], T.pr[:, :], T.u4[:, :], A.is_lt)
            xq = tt(T.xq[:, :], T.pr[:, :], T.u[:, :], A.add)
            need("v", w, zer)
            ppc, ends[s] = T.pp[:, :], T.pp[:, 7:8]
            pp = scan(ppc, T.w[:, :], T.zer[:, 0:8], A.add, A.max)
            g256 = ts(T.g256[:, :], T.w[:, :], 255.0, 1.0, A.mult, A.add)
            need("v", clist, mb)
            wm = tt(T.wm[:, :], T.w[:, :].indirect(T.clist[:, :]), T.maskb[:, :], A.mult)
        else:
            need("v", offs[s], hx, dw)
            gm = tt(T.gm[:, :], T.win[:, :].indirect(T.off[:, c:c + 8]), T.maskf[:, :], A.mult)
            need("v", dtw)
            wm = tt(T.wm[:, :], T.thw[:, :].indirect(T.off[:, c:c + 8]), T.hxm[:, :], A.is_ge)
            need("v", gm)
            e = scan(T.sc[:, :], T.blkf[:, :], T.gm[:, :], A.mult, A.add)
            need("v", wm)
            pp = scan(T.ppx[:, x + 16:x + 144], T.wm[:, :], T.zer[:, :], A.add, A.max)
            ppc, ends[s] = T.ppx[:, x + 31:x + 144:16], T.ppx[:, x + 143:x + 144]
            need("v", e)
            f3 = ts(T.f3[:, :], E, 2.0 ** -11, 0.500244140625, A.mult, A.add)
            need("v", slm)
            u = tt(T.u[:, :], T.slm[:, :], E, A.subtract)
            need("v", f3, h2)
            pr = tt(T.pr[:, :], T.f3[:, :], T.h2[:, :], A.mult)
        need("t", pp, lt)
        base = P(te.matmul(T.psb[:, 0:1], T.lt[:, :], ends[s], s == 0, True))
        if s == 0:
            segment(2)
            segment(3)
            need("v", xq, g256)
            y = tt(T.y[:, :], T.xq[:, :], T.g256[:, :], A.mult)
        else:
            need("t", i128, nid, zp, py)
            te.matmul(T.psr[:, 0:8], T.idn[:, :], ppc, True, False)
            te.matmul(T.psr[:, 0:8], T.nid[:, :], T.ppx[:, x + 15:x + 128:16], False, False)
            pg = P(te.matmul(T.psr[:, 0:8], T.ones[:, :], T.i128[:, :], False, True))
        need("v", base, con)
        prev = ts(T.off2[:, c:c + 8], ppc, T.psb[:, 0:1], None, A.add)
        if s > 0:
            need("v", pr, u)
            xq = tt(T.xq[:, :], T.pr[:, :], T.u[:, :], A.add)
        else:
            need("v", y)
            h2 = ts(T.h2[:, :], T.y[:, :], 2.0 ** -11, 2047.500244140625, A.mult, A.add)
            y2 = ts(T.ylo[:, :], T.y[:, :], 2047, None, A.bitwise_and)
        need("v", prev, wm, segc[2 * s + 1])
        t = tt(T.gb[:, :], T.bw[:, 0:1025 + 1024 * s].indirect(T.off2[:, c:c + 8]), T.wm[:, :], A.mult)
        if s > 0:
            need("v", xq, pg)
            py = y = tt(T.y[:, :], T.xq[:, :], T.psr[:, 0:8], A.mult)
        if s == 1:
            need("v", i2, pcf)
            permo = ts(T.permo[:, :], T.i2[:, :], T.pcf[:, 0:1], None, A.add)
        if s == 0:
            gather(3, 4)
            c3 = ts(T.c3[:, 0:1], T.ip[:, 0:1], 3, 1, A.arith_shift_right, A.bitwise_and)
        need("v", t, bb)
        t = scan(T.sb[:, :], T.blkb[:, :], T.gb[:, :], A.mult, A.add)
        if s == 3:
            need("v", t, y)
            xl = tt(T.xl[:, :], T.y[:, :], T.sb[:, 15:128:16], A.add)
            break
        if s > 0:
            need("v", y)
            y2 = ts(T.ylo[:, :], T.y[:, :], 2047, None, A.bitwise_and)
            h2 = ts(T.h2[:, :], T.y[:, :], 2.0 ** -11, 2047.500244140625, A.mult, A.add)
        else:
            need("v", c7)
            c16 = ts(T.c16[:, 0:1], T.c7[:, 0:1], 16.0, None, A.mult)
        need("v", t, y2)
        sl = tt(T.sl[:, :], T.ylo[:, :], T.sb[:, 15:128:16], A.add)
        if s == 0:
            need("v", c16, c3)
            pcf = tt(T.pcf[:, 0:1], T.c16[:, 0:1], T.c3[:, 0:1], A.add)
        need("v", h2, bm)
        hx = tt(T.hxm[:, :], T.h2[:, :].indirect(T.clist[:, :]), T.bmask[:, :], A.add)
        if s == 0:
            for q in range(16):
                dtw = dma("y", T.thw[q:128:16, :], T.land2[:, :, :], "dtw", a2, dow2)
            dlw = dma("y", T.lw[0:128:16, :], T.land3[:, :, :], "dlw", a3, dow3, lwf)
            segment(4)
            segment(5)
        elif s == 1:
            segment(6)
            segment(7)
            letters(0)
        else:
            letters(1)
            letters(2)
    outs = letters(3)

    dsy = dma("s", T.snd4[:, :, :], T.outs[0:128:16, :], "dsy", outs)
    dow4 = dma("s", T.land4[me, :, :], T.outs[16 * me:16 * me + 1, :], "dow4")
    need("g", dsy)
    a4 = send(T.snd4, T.land4, "a4")
    dla = dma("y", T.snd5[:, :, :], T.xl[:, :], "dla", xl)
    dow5 = dma("y", T.land5[me, :, :], T.xl[16 * me:16 * me + 16, :], "dow5")
    need("g", dla)
    a5 = send(T.snd5, T.land5, "a5")
    dma("s", T.syms[:, :], T.land4[:, :, :], "fsy", a4, dow4)
    dma("y", T.last[:, :], T.land5[:, :, :], "fla", a5, dow5)
    for sem in sorted(cnt):
        if waited.get(sem, 0) < cnt[sem]:
            need("g", (sem, cnt[sem]))
